import numpy as np
import ml_dtypes


def mxq(x, axis, fmt="e4m3"):
    dtype, down = {"e4m3": (ml_dtypes.float8_e4m3fn, 7), "e5m2": (ml_dtypes.float8_e5m2, 14)}[fmt]
    v = np.moveaxis(np.asarray(x, np.float32).astype(ml_dtypes.bfloat16).astype(np.float64), axis, -1)
    blocks = v.reshape(v.shape[:-1] + (-1, 32))
    amax = np.abs(blocks).max(-1, keepdims=True)
    byte = np.maximum(np.where(amax > 0, np.frexp(amax)[1] - 1 + 127, 0) - down, 1)
    scale = np.exp2(byte - 127.0)
    codes = (blocks / scale).astype(np.float32).astype(dtype).astype(np.float64)
    return np.moveaxis((codes * scale).reshape(v.shape), -1, axis)


WIDE = False


def mx_kscale(k):
    if not WIDE:
        return np.ones(k)
    levels = np.array([30, -30])
    if k % 512:
        return np.exp2(np.random.permutation(np.resize(levels, k // 32))).repeat(32)
    a = np.empty((k // 512, 16))
    for p in range(k // 512):
        a[p, :8] = np.random.permutation(np.resize(levels, 8))
        for g in range(8):
            far = levels[np.abs(levels - a[p, g]) >= 10]
            a[p, g + 8] = far[np.random.randint(len(far))]
    return np.exp2(a.ravel()).repeat(32)


BF16 = ml_dtypes.bfloat16


def bf(x):
    return np.asarray(x, np.float32).astype(BF16)


def f64(x):
    return np.asarray(x).astype(np.float64)


E2M1 = np.array([0.0, 0.5, 1.0, 1.5, 2.0, 3.0, 4.0, 6.0, -0.0, -0.5, -1.0, -1.5, -2.0, -3.0, -4.0, -6.0])


def pack_weight(w, fmt):
    k, n = w.shape
    w = f64(bf(w)).reshape(k // 32, 32, n)
    amax = np.abs(w).max(1)
    if fmt == "e4m3":
        byte = np.frexp(amax)[1] - 1 + 127 - 7
    else:
        mant, ex = np.frexp(amax / 6.0)
        byte = np.where(mant > 0.5, ex, ex - 1) + 127
    byte = np.clip(np.where(amax > 0, byte, 1), 1, 254)
    scaled = (w * np.exp2(127.0 - byte)[:, None, :]).reshape(k, n).astype(np.float32)
    by_word = np.ascontiguousarray(scaled.reshape(k // 512, 128, 4, n).transpose(0, 1, 3, 2))
    if fmt == "e4m3":
        words = by_word.astype(ml_dtypes.float8_e4m3fn).view(np.uint8)
    else:
        c = by_word.astype(ml_dtypes.float4_e2m1fn).view(np.uint8) & 0xF
        words = c[..., 0::2] | (c[..., 1::2] << 4)
    return np.ascontiguousarray(words), np.ascontiguousarray(byte.astype(np.uint8).reshape(k // 512, 16, n))


def unpack_weight(words, scales, fmt):
    g, p, n, _ = words.shape
    if fmt == "e4m3":
        vals = np.ascontiguousarray(words).view(ml_dtypes.float8_e4m3fn).astype(np.float64)
    else:
        nib = np.empty((g, p, n, 4), np.uint8)
        nib[..., 0::2] = words & 0xF
        nib[..., 1::2] = words >> 4
        vals = E2M1[nib]
    vals = vals * np.repeat(np.exp2(scales.astype(np.float64) - 127.0), 8, axis=1)[..., None]
    return vals.transpose(0, 1, 3, 2).reshape(g * 512, n)
def pack4(w):
    words, scales = pack_weight(w, "e2m1")
    return words.reshape(words.shape[0], 128, -1), scales


def unpack4(words, scales):
    return unpack_weight(words.reshape(words.shape[0], 128, -1, 2), scales, "e2m1")


M, K, F, U, S = 1024, 2048, 1024, 128, 16


def setup_inputs():
    s = mx_kscale(K)
    t = mx_kscale(F)
    w = np.random.standard_normal((K, F)) / np.sqrt(K) / s[:, None] * t
    w_words, w_scales = pack4(w)
    return {"x": bf(np.random.standard_normal((M, K)) * s),
            "w_words": w_words,
            "w_scales": w_scales,
            "b": bf(0.3 * np.random.standard_normal(F) * t),
            "users": bf(np.random.standard_normal((F, U)) / np.sqrt(F) / t[:, None]),
            "selected": bf(np.random.standard_normal((F, U * S)) / np.sqrt(F) / t[:, None]),
            "lam": bf(0.5 + 0.1 * np.random.standard_normal(U))}


def reference(x, w_words, w_scales, b, users, selected, lam):
    h = mxq(f64(x), 1, "e4m3") @ unpack4(w_words, w_scales)
    h = np.maximum(h + f64(b), 0.0)
    hq = mxq(h, 1, "e5m2")
    rel = hq @ mxq(f64(users), 0, "e4m3")
    sim = hq @ mxq(f64(selected), 0, "e4m3")
    red = sim.reshape(M, U, S).max(axis=2)
    return rel - f64(lam) * red

@@ -1,0 +1,437 @@
+from contextlib import ExitStack
+
+import concourse.mybir as mybir
+from concourse.masks import make_identity
+
+F32 = mybir.dt.float32
+BF16 = mybir.dt.bfloat16
+I32 = mybir.dt.int32
+U32 = mybir.dt.uint32
+U8 = mybir.dt.uint8
+E4M3 = mybir.dt.float8_e4m3fn_x4
+E5M2 = mybir.dt.float8_e5m2_x4
+E2M1 = mybir.dt.float4_e2m1fn_x4
+ALU = mybir.AluOpType
+ACT = mybir.ActivationFunctionType
+
+TOKENS, K, F, USERS, SLATE = 1024, 2048, 1024, 128, 16
+FLOPS = 2 * TOKENS * K * F + 2 * TOKENS * F * (USERS + USERS * SLATE)
+
+P = 128
+SLABS = 2
+R = 4
+G = 4
+H = 2
+T = 4
+N = 512
+
+
+def tile_marginal_relevance_slates_s9_kernel(tc, x, w_words, w_scales, b, users, selected, lam, out):
+    nc = tc.nc
+    with ExitStack() as ctx:
+        keep = ctx.enter_context(tc.tile_pool(name="keep", bufs=1))
+        work = ctx.enter_context(tc.tile_pool(name="work", bufs=2))
+        psum = ctx.enter_context(tc.psum_pool(name="psum", bufs=1))
+        ctx.enter_context(tc.manual_schedule())
+
+        x_view = x.rearrange("(s p r) k -> s p r k", s=SLABS, r=R)
+        x_raw = {}
+
+        def load_x(s, gp, rp):
+            t = keep.tile([P, 2, 1024], BF16, name="xraw_%d_%d_%d" % (s, gp, rp))
+            nc.sync.dma_start(out=t[:], in_=x_view[s][:, 2 * rp : 2 * rp + 2, 1024 * gp : 1024 * gp + 1024])
+            x_raw[s, gp, rp] = t
+
+        w_raw = keep.tile([P, H, G * 1024], U8, name="w_raw", align_bytes=64)
+        w_perm = keep.tile([P, H, G * 1024], U8, name="w_perm", align_bytes=64)
+        ws_raw = keep.tile([P, G * 1024], U8, name="ws_raw", align_bytes=64)
+        ws_perm = keep.tile([P, G * 1024], U8, name="ws_perm", align_bytes=64)
+        w_view = w_words.bitcast(I32).rearrange("g p (h n) -> h p g n", h=H)
+        ws_view = w_scales.bitcast(I32).rearrange("g r n -> r g n")
+        ws_raw_i = ws_raw[:].bitcast(I32).rearrange("p (g n) -> p g n", g=G)
+
+        def load_w(h):
+            nc.sync.dma_start(out=w_raw[:, h, :].bitcast(I32).rearrange("p (g n) -> p g n", g=G), in_=w_view[h])
+
+        def load_ws():
+            for q in range(4):
+                nc.sync.dma_start(out=ws_raw_i[32 * q : 32 * q + 4], in_=ws_view[4 * q : 4 * q + 4])
+
+        rows = keep.tile([P, P], BF16, name="rows")
+        sel_view = selected.rearrange("(h b t i) c -> h t b i c", h=H, t=T, i=8)
+        use_view = users.rearrange("(h b t i) c -> h t b i c", h=H, t=T, i=8)
+        sel_raw = [keep.tile([P, T, 2048], BF16, name="sel_raw%d" % h) for h in range(H)]
+        use_raw = [keep.tile([P, T, USERS], BF16, name="use_raw%d" % h) for h in range(H)]
+
+        def load_selected(h, half):
+            c = slice(1024 * half, 1024 * half + 1024)
+            for t in range(T):
+                nc.sync.dma_start(out=sel_raw[h][:, t, c], in_=sel_view[h, t][:, :, c])
+
+        def load_rows():
+            for h in range(H):
+                nc.sync.dma_start(out=rows[4 * h : 4 * h + 4, :].rearrange("t (b i) -> t b i", i=8), in_=b_view[h])
+            nc.sync.dma_start(out=rows[8:9, :], in_=lam.rearrange("(o u) -> o u", o=1))
+
+        nc.vector.memset(ws_raw[:].bitcast(I32), 0)
+        nc.vector.memset(rows[:], 0.0)
+        ident = keep.tile([P, P], F32, name="ident")
+        make_identity(nc, ident[:])
+        ident_b = keep.tile([P, P], BF16, name="ident_b")
+        bias = keep.tile([P, 16], F32, name="bias")
+        nlam = keep.tile([P, 1], F32, name="nlam")
+        warm = keep.tile([P, 1], F32, name="warm")
+        nc.vector.memset(warm[:], 0.0)
+        nc.scalar.activation(out=warm[:], in_=warm[:], func=ACT.Relu)
+        nc.vector.tensor_copy(out=ident_b[:], in_=ident[:])
+
+        b_view = b.rearrange("(h b t i) -> h t b i", h=H, t=T, i=8)
+        load_x(0, 0, 0)
+        load_x(0, 0, 1)
+        load_w(0)
+        load_ws()
+        load_x(0, 1, 0)
+        load_x(0, 1, 1)
+        load_rows()
+        load_selected(0, 0)
+        load_w(1)
+        load_selected(0, 1)
+        load_x(1, 0, 0)
+        load_x(1, 0, 1)
+        load_x(1, 1, 0)
+        load_x(1, 1, 1)
+        load_selected(1, 0)
+        load_selected(1, 1)
+        for h in range(H):
+            for t in range(T):
+                nc.sync.dma_start(out=use_raw[h][:, t, :], in_=use_view[h, t])
+
+        steps = {}
+
+        def step(name, needs):
+            def wrap(fn):
+                steps[name] = (needs, fn)
+
+            return wrap
+
+        def make_wperm(h, t):
+            src = w_raw[:, h, :].bitcast(I32).rearrange("p (g b t w) -> p g b t w", b=16, t=T, w=4)
+            dst = w_perm[:, h, :].bitcast(I32).rearrange("p (g t b w) -> p g t b w", b=16, t=T, w=4)
+            nc.vector.tensor_copy(out=dst[:, :, t], in_=src[:, :, :, t])
+
+        def make_wsperm(t):
+            s_src = ws_raw[:].bitcast(I32).rearrange("p (q b t w) -> p q b t w", b=16, t=T, w=2)
+            s_dst = ws_perm[:].bitcast(I32).rearrange("p (q t b w) -> p q t b w", b=16, t=T, w=2)
+            nc.vector.tensor_copy(out=s_dst[:, :, t], in_=s_src[:, :, :, t])
+
+        x_codes = [keep.tile([P, G * N], U32, name="x_codes%d" % s, align_bytes=64) for s in range(SLABS)]
+        x_scales = [keep.tile([P, G * N], U8, name="x_scales%d" % s, align_bytes=64) for s in range(SLABS)]
+        x_in = {}
+        x_bank = {}
+
+        def tr(s, g, rp):
+            words = x_raw[s, g // 2, rp][:].rearrange("p r k -> p (r k)").bitcast(F32)
+            bank = psum.tile([P, N], F32, name="tr", bufs=TRB)
+            x_bank[s, g, rp] = bank
+            for r in range(2):
+                for u in range(2):
+                    w0 = 512 * r + 256 * (g % 2) + u
+                    c0 = 256 * r + 128 * u
+                    nc.tensor.transpose(bank[:, c0 : c0 + 128], words[:, w0 : w0 + 255 : 2], ident[:])
+
+        def xc(s, g, rp, e):
+            if (s, g) not in x_in:
+                x_in[s, g] = work.tile([P, N * T], BF16, name="x_in", align_bytes=64, bufs=4)
+            dst = x_in[s, g][:].bitcast(F32).rearrange("p (r n u) -> p r n u", r=R, u=2)[:, 2 * rp : 2 * rp + 2]
+            src = x_bank[s, g, rp][:].rearrange("p (r u n) -> p r n u", r=2, u=2)
+            if e == "v":
+                nc.vector.tensor_copy(out=dst, in_=src)
+            else:
+                nc.scalar.copy(out=dst, in_=src)
+
+        def xq(s, g):
+            c = slice(g * N, (g + 1) * N)
+            nc.vector.quantize_mx(out=x_codes[s][:, c].bitcast(E4M3), scales=x_scales[s][:, c], in_=x_in[s, g][:])
+
+        acc1 = {}
+        h_raw = {}
+        h_in = {}
+
+        def mx1(s, h, t, g):
+            if g == 0:
+                acc1[s, h, t] = psum.tile([P, N], F32, name="acc", bufs=ACB)
+            q = g * T + t
+            qs = (g * H + h) * T + t
+            c = slice(g * N, (g + 1) * N)
+            nc.tensor.matmul_mx(
+                out=acc1[s, h, t][:],
+                lhsT=w_perm[:, h, 256 * q : 256 * q + 256].bitcast(E2M1),
+                lhsT_scale=ws_perm[:, 128 * qs : 128 * qs + 128],
+                rhs=x_codes[s][:, c].bitcast(E4M3),
+                rhs_scale=x_scales[s][:, c],
+                start=(g == 0),
+                stop=(g == G - 1),
+            )
+
+        def relu(s, h, t):
+            if (s, h) not in h_raw:
+                h_raw[s, h] = work.tile([P, T, N], BF16, name="h_raw", bufs=2)
+            nc.scalar.activation(
+                out=h_raw[s, h][:, t, :], in_=acc1[s, h, t][:], func=ACT.Relu, bias=bias[:, h * T + t : h * T + t + 1], scale=1.0
+            )
+
+        h_codes = [keep.tile([P, H * N], U32, name="h_codes%d" % s, align_bytes=64) for s in range(SLABS)]
+        h_scales = [keep.tile([P, H * N], U8, name="h_scales%d" % s, align_bytes=64) for s in range(SLABS)]
+
+        def hi(s, h):
+            h_in[s, h] = work.tile([P, N, T], BF16, name="h_in", align_bytes=64, bufs=2)
+            nc.vector.tensor_copy(out=h_in[s, h][:], in_=h_raw[s, h][:].rearrange("p t n -> p n t"))
+
+        def hq(s, h):
+            c = slice(h * N, (h + 1) * N)
+            nc.vector.quantize_mx(
+                out=h_codes[s][:, c].bitcast(E5M2), scales=h_scales[s][:, c], in_=h_in[s, h][:].rearrange("p n t -> p (n t)")
+            )
+
+        sel_codes = [keep.tile([P, SLATE * USERS], U32, name="sel_codes%d" % h, align_bytes=64) for h in range(H)]
+        sel_scales = [keep.tile([P, SLATE * USERS], U8, name="sel_scales%d" % h, align_bytes=64) for h in range(H)]
+        use_codes = [keep.tile([P, USERS], U32, name="use_codes%d" % h, align_bytes=64) for h in range(H)]
+        use_scales = [keep.tile([P, USERS], U8, name="use_scales%d" % h, align_bytes=64) for h in range(H)]
+        s_in = {}
+
+        def si(h, k, half, e):
+            if (h, k) not in s_in:
+                s_in[h, k] = work.tile([P, 4, USERS, T], BF16, name="s_in", align_bytes=64, bufs=8)
+            u = slice(64 * half, 64 * half + 64)
+            dst = s_in[h, k][:].rearrange("p j u t -> p u j t")[:, u]
+            src = sel_raw[h][:].rearrange("p t (u j) -> p u j t", j=SLATE)[:, u, 4 * k : 4 * k + 4]
+            if e == "v":
+                nc.vector.tensor_copy(out=dst, in_=src)
+            elif e == "g":
+                nc.gpsimd.tensor_scalar(out=dst, in0=src, scalar1=1.0, scalar2=0.0, op0=ALU.mult, op1=ALU.add)
+            else:
+                nc.scalar.copy(out=dst, in_=src)
+
+        def sq(h, k):
+            c = slice(512 * k, 512 * k + 512)
+            nc.vector.quantize_mx(
+                out=sel_codes[h][:, c].bitcast(E4M3), scales=sel_scales[h][:, c], in_=s_in[h, k][:].rearrange("p j u t -> p (j u t)")
+            )
+
+        u_in = {}
+
+        def ui(h):
+            u_in[h] = work.tile([P, USERS, T], BF16, name="u_in", align_bytes=64, bufs=2)
+            nc.vector.tensor_copy(out=u_in[h][:], in_=use_raw[h][:].rearrange("p t u -> p u t"))
+
+        def uq(h):
+            nc.vector.quantize_mx(
+                out=use_codes[h][:].bitcast(E4M3), scales=use_scales[h][:], in_=u_in[h][:].rearrange("p u t -> p (u t)")
+            )
+
+        acc2 = {}
+        best = {}
+        rel = {}
+        res_t = {}
+
+        def mx2(s, j):
+            acc2[s, j] = psum.tile([P, N], F32, name="acc", bufs=ACB)
+            codes, scales, c = (use_codes, use_scales, slice(0, USERS)) if j == "u" else (sel_codes, sel_scales, slice(USERS * j, USERS * j + USERS))
+            for h in range(H):
+                m = slice(h * N, (h + 1) * N)
+                nc.tensor.matmul_mx(
+                    out=acc2[s, j][:],
+                    lhsT=codes[h][:, c].bitcast(E4M3),
+                    lhsT_scale=scales[h][:, c],
+                    rhs=h_codes[s][:, m].bitcast(E5M2),
+                    rhs_scale=h_scales[s][:, m],
+                    start=(h == 0),
+                    stop=(h == H - 1),
+                )
+
+        def cp2(s, j):
+            into = rel if j == "u" else best
+            into[s] = work.tile([P, N], F32, name="rel" if j == "u" else "best", bufs=2)
+            nc.scalar.copy(out=into[s][:], in_=acc2[s, j][:])
+
+        def mxx(s, j, c0, c1):
+            d = best[s][:, c0:c1]
+            nc.vector.tensor_tensor(out=d, in0=acc2[s, j][:, c0:c1], in1=d, op=ALU.max)
+
+        def fin(s, c0, c1):
+            if s not in res_t:
+                res_t[s] = work.tile([P, N], F32, name="res_t", bufs=2)
+            nc.vector.scalar_tensor_tensor(
+                out=res_t[s][:, c0:c1], in0=best[s][:, c0:c1], scalar=nlam[:], in1=rel[s][:, c0:c1], op0=ALU.mult, op1=ALU.add
+            )
+
+        out_view = out.rearrange("(s p r) u -> s p r u", s=SLABS, r=R)
+        o_bank = {}
+
+        def otr(s, r0, r1):
+            o_bank[s, r0] = psum.tile([P, N], F32, name="tr", bufs=TRB)
+            for r in range(r0, r1):
+                nc.tensor.transpose(o_bank[s, r0][:, 128 * (r - r0) : 128 * (r - r0) + 128], res_t[s][:, 128 * r : 128 * r + 128], ident[:])
+
+        def oc(s, r0, r1, e):
+            res = work.tile([P, r1 - r0, USERS], F32, name="res%d" % (r1 - r0), bufs=2)
+            d, i = res[:].rearrange("p r u -> p (r u)"), o_bank[s, r0][:, : 128 * (r1 - r0)]
+            if e == "v":
+                nc.vector.tensor_copy(out=d, in_=i)
+            else:
+                nc.scalar.copy(out=d, in_=i)
+            nc.sync.dma_start(out=out_view[s][:, r0:r1], in_=res[:])
+
+        def btr():
+            x_bank["b"] = psum.tile([P, P], BF16, name="tr", bufs=TRB)
+            nc.tensor.transpose(x_bank["b"][:], rows[:], ident_b[:])
+
+        def bcopy():
+            nc.vector.tensor_copy(out=bias[:, 0:9], in_=x_bank["b"][:, 0:9])
+            nc.vector.tensor_scalar(out=nlam[:], in0=x_bank["b"][:, 8:9], scalar1=-1.0, scalar2=None, op0=ALU.mult)
+
+
+        pe, act, dve, pool = [], [], [], []
+        TRB, ACB = 4, 4
+
+        def relus(s, h, t0):
+            return [("relu", s, h, t0), ("relu", s, h, t0 + 1)]
+
+        def pair(s, h, t0):
+            return [("mx1", s, h, t, g) for t in (t0, t0 + 1) for g in range(G)]
+
+        def trs(s, gp):
+            return [("tr", s, g, rp) for rp in range(2) for g in (2 * gp, 2 * gp + 1)]
+
+        pe += trs(0, 0) + trs(0, 1) + [("btr",)]
+        pe += [("mx1", 0, 0, t, g) for g in range(G) for t in (0, 1)]
+        pe += pair(0, 0, 2) + pair(0, 1, 0)
+        pe += trs(1, 0) + pair(0, 1, 2) + trs(1, 1)
+        pe += [("mx1", 1, 0, t, g) for g in range(G) for t in (0, 1)]
+        seq = [0, 1, 2, 3, "u"] + list(range(4, 16))
+        EARLY = [0, 2, 3, 3]
+        LEAD = 8
+        pe += [("mx2", 0, j) for j in seq[0:0]]
+        pe += pair(1, 0, 2) + [("mx2", 0, j) for j in seq[0:2]]
+        pe += pair(1, 1, 0) + [("mx2", 0, j) for j in seq[2:5]]
+        pe += pair(1, 1, 2)
+        two = [(0, j) for j in seq[:5]]
+        rest = []
+        for i in range(5, 17 + LEAD):
+            if i < 17:
+                rest.append((0, seq[i]))
+            if i >= LEAD:
+                rest.append((1, seq[i - LEAD]))
+        two += rest
+        for i, n in enumerate(rest):
+            pe += [("mx2",) + n] + ([("otr", 0, 0, 4)] if i == len(rest) - 3 else [])
+        pe += [("otr", 1, 0, 2), ("otr", 1, 2, 4)]
+
+        act += [("xc", 0, 2 * gp, rp, "s") for gp in range(2) for rp in range(2)]
+        act += [("si", 0, 0, 0, "s")] + relus(0, 0, 0)
+        act += [("si", 0, 0, 1, "s")] + relus(0, 0, 2)
+        act += [("si", 0, 3, 1, "s")] + relus(0, 1, 0)
+        act += [("xc", 1, 0, 0, "s"), ("xc", 1, 1, 0, "s"), ("xc", 1, 0, 1, "s")] + relus(0, 1, 2)
+        act += [("xc", 1, 2, 0, "s"), ("xc", 1, 3, 0, "s"), ("xc", 1, 2, 1, "s"), ("si", 1, 0, 0, "s"), ("si", 1, 0, 1, "s")] + relus(1, 0, 0)
+        act += [("si", 1, 1, 0, "s")] + relus(1, 0, 2)
+        act += [("cp2", 0, 0), ("si", 1, 1, 1, "s")] + relus(1, 1, 0)
+        act += [("cp2", 0, "u"), ("si", 1, 2, 1, "s")] + relus(1, 1, 2)
+        act += [("si", 1, 3, 0, "s"), ("si", 1, 3, 1, "s"), ("cp2", 1, 0)]
+        act += [("cp2", 1, "u"), ("oc", 0, 0, 4, "s")]
+        act += [("oc", 1, 0, 2, "s"), ("oc", 1, 2, 4, "s")]
+
+        dve += [("xc", 0, 1, 0, "v")]
+        dve += [("xc", 0, 1, 1, "v")]
+        dve += [("wp", 0, t) for t in range(4)] + [("wsp", t) for t in range(4)]
+        dve += [("xq", 0, 0), ("xq", 0, 1), ("xc", 0, 3, 0, "v"), ("xc", 0, 3, 1, "v"), ("bcopy",), ("xq", 0, 2), ("xq", 0, 3)]
+        dve += [("si", 0, 1, 0, "v"), ("si", 0, 2, 0, "v")]
+        dve += [("wp", 1, t) for t in range(4)]
+        dve += [("si", 0, 3, 0, "v"), ("si", 0, 1, 1, "v"), ("si", 0, 2, 1, "v"), ("sq", 0, 1), ("hi", 0, 0), ("sq", 0, 0), ("hq", 0, 0)]
+        dve += [("xc", 1, 1, 1, "v"), ("sq", 0, 2), ("xq", 1, 0), ("xq", 1, 1), ("sq", 0, 3)]
+        dve += [("si", 1, 2, 0, "v"), ("xc", 1, 3, 1, "v"), ("xq", 1, 2), ("xq", 1, 3), ("hi", 0, 1)]
+        dve += [("ui", 0), ("hq", 0, 1), ("ui", 1), ("uq", 0), ("uq", 1), ("sq", 1, 0)]
+        mm = {}
+        full = {}
+        HALF = {(0, 2), (0, 3), (0, 4), (0, 5), (0, 6)} | {(1, j) for j in range(8, 16)}
+        for s, j in two:
+            if j not in ("u", 0):
+                mm[s, j] = [("mxx", s, j, 0, 256), ("mxx", s, j, 256, 512)] if (s, j) in HALF else [("mxx", s, j, 0, 512)]
+        dve += mm[0, 1] + [("hi", 1, 0), ("sq", 1, 1), ("hq", 1, 0)] + mm[0, 2] + mm[0, 3]
+        dve += [("sq", 1, 2), ("hi", 1, 1)] + mm[0, 4] + [("hq", 1, 1)] + mm[0, 5] + mm[0, 6] + [("sq", 1, 3)]
+        for s, j in rest:
+            if j in ("u", 0) or (s == 0 and j < 7):
+                continue
+            dve += mm[s, j]
+            if (s, j) == (1, 9):
+                dve += [("fin", 0, 0, 512)]
+        dve += [("fin", 1, 0, 256), ("fin", 1, 256, 512)]
+
+        fns = dict(wp=make_wperm, wsp=make_wsperm, tr=tr, xc=xc, xq=xq, mx1=mx1, relu=relu, hi=hi, hq=hq, si=si, sq=sq, ui=ui, uq=uq, mx2=mx2, cp2=cp2, mxx=mxx, fin=fin, otr=otr, oc=oc, btr=btr, bcopy=bcopy)
+
+        def strip(n):
+            return n[:-1] if n[0] in ("xc", "si", "oc") else n
+
+        tr_ring, acc_ring = [], []
+        for n in pe:
+            if n[0] == "tr":
+                tr_ring.append((n, [("xc",) + n[1:]]))
+            elif n[0] == "btr":
+                tr_ring.append((n, [("bcopy",)]))
+            elif n[0] == "otr":
+                tr_ring.append((n, [("oc",) + n[1:]]))
+            elif n[0] == "mx1" and n[4] == 0:
+                acc_ring.append((n, [("relu",) + n[1:4]]))
+            elif n[0] == "mx2":
+                acc_ring.append((n, [("cp2",) + n[1:]] if n[2] in ("u", 0) else [m for m in dve if m[:3] == ("mxx", n[1], n[2])]))
+        ring_need = {}
+        for ring, bufs in ((tr_ring, TRB), (acc_ring, ACB)):
+            for i in range(bufs, len(ring)):
+                ring_need[ring[i][0]] = ring[i - bufs][1]
+
+        def needs(n):
+            k = n[0]
+            r = list(ring_need.get(n, []))
+            if k == "xc":
+                r += [("tr",) + n[1:4]] + ([("xq", 0, n[2])] if n[1] == 1 else [])
+            elif k == "xq":
+                r += [("xc", n[1], n[2], 0), ("xc", n[1], n[2], 1)]
+            elif k == "mx1":
+                r += [("xq", n[1], n[4]), ("wp", n[2], n[3]), ("wsp", n[3])]
+            elif k == "relu":
+                r += [("mx1", n[1], n[2], n[3], 3), ("bcopy",)] + ([("hi", 0, n[2])] if n[1] == 1 else [])
+            elif k == "hi":
+                r += [("relu", n[1], n[2], t) for t in range(T)] + ([("hq", 0, n[2])] if n[1] == 1 else [])
+            elif k == "hq":
+                r += [("hi", n[1], n[2])]
+            elif k == "sq":
+                r += [("si", n[1], n[2], 0), ("si", n[1], n[2], 1)]
+            elif k == "uq":
+                r += [("ui", n[1])]
+            elif k == "mx2":
+                r += [("hq", n[1], 0), ("hq", n[1], 1)]
+                r += [("uq", 0), ("uq", 1)] if n[2] == "u" else [("sq", 0, n[2] // 4), ("sq", 1, n[2] // 4)]
+            elif k == "cp2":
+                r += [("mx2", n[1], n[2])]
+            elif k == "mxx":
+                r += [("mx2", n[1], n[2]), ("cp2", n[1], 0)]
+            elif k == "fin":
+                r += [("cp2", n[1], "u")]
+            elif k == "otr":
+                r += [("fin", n[1], 128 * n[2], 128 * n[3])]
+            elif k == "oc":
+                r += [("otr", n[1], n[2], n[3])]
+            elif k == "bcopy":
+                r += [("btr",)]
+            return r
+
+        done = set()
+        order = [list(pe), list(act), list(dve), list(pool)]
+        while any(order):
+            moved = False
+            for q in order:
+                while q and all(n in done for n in needs(q[0])):
+                    name = q.pop(0)
+                    fns[name[0]](*name[1:])
+                    done.add(strip(name))
+                    moved = True
+            assert moved, [q[0] for q in order if q]

@@ -13,6 +13,7 @@ E5M2 = mybir.dt.float8_e5m2_x4
 E2M1 = mybir.dt.float4_e2m1fn_x4
 ALU = mybir.AluOpType
 ACT = mybir.ActivationFunctionType
+AXES = mybir.AxisListType
 
 TOKENS, K, F, USERS, SLATE = 1024, 2048, 1024, 128, 16
 FLOPS = 2 * TOKENS * K * F + 2 * TOKENS * F * (USERS + USERS * SLATE)
@@ -75,21 +76,23 @@ def tile_marginal_relevance_slates_s9_kernel(tc, x, w_words, w_scales, b, users,
 
         nc.vector.memset(ws_raw[:].bitcast(I32), 0)
         nc.vector.memset(rows[:], 0.0)
-        ident = keep.tile([P, P], F32, name="ident")
-        make_identity(nc, ident[:])
         ident_b = keep.tile([P, P], BF16, name="ident_b")
         bias = keep.tile([P, 16], F32, name="bias")
-        nlam = keep.tile([P, 1], F32, name="nlam")
+        lam_row = keep.tile([P, USERS], F32, name="lam_row")
+        zero = keep.tile([P, N], BF16, name="zero")
+        nc.gpsimd.memset(zero[:], 0.0)
+        ident = keep.tile([P, P], F32, name="ident")
+        make_identity(nc, ident[:])
         warm = keep.tile([P, 1], F32, name="warm")
         nc.vector.memset(warm[:], 0.0)
         nc.scalar.activation(out=warm[:], in_=warm[:], func=ACT.Relu)
         nc.vector.tensor_copy(out=ident_b[:], in_=ident[:])
 
         b_view = b.rearrange("(h b t i) -> h t b i", h=H, t=T, i=8)
-        load_x(0, 0, 0)
-        load_x(0, 0, 1)
         load_w(0)
         load_ws()
+        load_x(0, 0, 0)
+        load_x(0, 0, 1)
         load_x(0, 1, 0)
         load_x(0, 1, 1)
         load_rows()
@@ -98,9 +101,9 @@ def tile_marginal_relevance_slates_s9_kernel(tc, x, w_words, w_scales, b, users,
         load_selected(0, 1)
         load_x(1, 0, 0)
         load_x(1, 0, 1)
+        load_selected(1, 0)
         load_x(1, 1, 0)
         load_x(1, 1, 1)
-        load_selected(1, 0)
         load_selected(1, 1)
         for h in range(H):
             for t in range(T):
@@ -114,15 +117,17 @@ def tile_marginal_relevance_slates_s9_kernel(tc, x, w_words, w_scales, b, users,
 
             return wrap
 
-        def make_wperm(h, t):
-            src = w_raw[:, h, :].bitcast(I32).rearrange("p (g b t w) -> p g b t w", b=16, t=T, w=4)
+        def wp(h):
+            src = w_raw[:, h, :].bitcast(I32).rearrange("p (g b t w) -> p g t b w", b=16, t=T, w=4)
             dst = w_perm[:, h, :].bitcast(I32).rearrange("p (g t b w) -> p g t b w", b=16, t=T, w=4)
-            nc.vector.tensor_copy(out=dst[:, :, t], in_=src[:, :, :, t])
+            for t in range(T):
+                nc.vector.tensor_copy(out=dst[:, :, t], in_=src[:, :, t])
 
-        def make_wsperm(t):
-            s_src = ws_raw[:].bitcast(I32).rearrange("p (q b t w) -> p q b t w", b=16, t=T, w=2)
-            s_dst = ws_perm[:].bitcast(I32).rearrange("p (q t b w) -> p q t b w", b=16, t=T, w=2)
-            nc.vector.tensor_copy(out=s_dst[:, :, t], in_=s_src[:, :, :, t])
+        def wsp():
+            src = ws_raw[:].bitcast(I32).rearrange("p (q b t w) -> p q t b w", b=16, t=T, w=2)
+            dst = ws_perm[:].bitcast(I32).rearrange("p (q t b w) -> p q t b w", b=16, t=T, w=2)
+            for t in range(T):
+                nc.vector.tensor_copy(out=dst[:, :, t], in_=src[:, :, t])
 
         x_codes = [keep.tile([P, G * N], U32, name="x_codes%d" % s, align_bytes=64) for s in range(SLABS)]
         x_scales = [keep.tile([P, G * N], U8, name="x_scales%d" % s, align_bytes=64) for s in range(SLABS)]
@@ -201,28 +206,29 @@ def tile_marginal_relevance_slates_s9_kernel(tc, x, w_words, w_scales, b, users,
 
         def si(h, k, half, e):
             if (h, k) not in s_in:
-                s_in[h, k] = work.tile([P, 4, USERS, T], BF16, name="s_in", align_bytes=64, bufs=8)
-            u = slice(64 * half, 64 * half + 64)
-            dst = s_in[h, k][:].rearrange("p j u t -> p u j t")[:, u]
-            src = sel_raw[h][:].rearrange("p t (u j) -> p u j t", j=SLATE)[:, u, 4 * k : 4 * k + 4]
+                s_in[h, k] = work.tile([P, N, T], BF16, name="s_in", align_bytes=64, bufs=8)
+            dst = s_in[h, k][:, 256 * half : 256 * half + 256]
+            src = sel_raw[h][:, :, 512 * k + 256 * half : 512 * k + 256 * half + 256].rearrange("p t c -> p c t")
             if e == "v":
                 nc.vector.tensor_copy(out=dst, in_=src)
-            elif e == "g":
-                nc.gpsimd.tensor_scalar(out=dst, in0=src, scalar1=1.0, scalar2=0.0, op0=ALU.mult, op1=ALU.add)
             else:
                 nc.scalar.copy(out=dst, in_=src)
 
         def sq(h, k):
             c = slice(512 * k, 512 * k + 512)
             nc.vector.quantize_mx(
-                out=sel_codes[h][:, c].bitcast(E4M3), scales=sel_scales[h][:, c], in_=s_in[h, k][:].rearrange("p j u t -> p (j u t)")
+                out=sel_codes[h][:, c].bitcast(E4M3), scales=sel_scales[h][:, c], in_=s_in[h, k][:].rearrange("p c t -> p (c t)")
             )
 
         u_in = {}
 
-        def ui(h):
+        def ui(h, e):
             u_in[h] = work.tile([P, USERS, T], BF16, name="u_in", align_bytes=64, bufs=2)
-            nc.vector.tensor_copy(out=u_in[h][:], in_=use_raw[h][:].rearrange("p t u -> p u t"))
+            src = use_raw[h][:].rearrange("p t u -> p u t")
+            if e == "v":
+                nc.vector.tensor_copy(out=u_in[h][:], in_=src)
+            else:
+                nc.scalar.copy(out=u_in[h][:], in_=src)
 
         def uq(h):
             nc.vector.quantize_mx(
@@ -230,57 +236,75 @@ def tile_marginal_relevance_slates_s9_kernel(tc, x, w_words, w_scales, b, users,
             )
 
         acc2 = {}
-        best = {}
+        rel_t = {}
         rel = {}
-        res_t = {}
+        red = [keep.tile([P, R, USERS], F32, name="red%d" % s) for s in range(SLABS)]
+        res = [keep.tile([P, R, USERS], F32, name="res%d" % s) for s in range(SLABS)]
 
-        def mx2(s, j):
-            acc2[s, j] = psum.tile([P, N], F32, name="acc", bufs=ACB)
-            codes, scales, c = (use_codes, use_scales, slice(0, USERS)) if j == "u" else (sel_codes, sel_scales, slice(USERS * j, USERS * j + USERS))
+        def mxu(s):
+            acc2[s, "u"] = psum.tile([P, N], F32, name="acc", bufs=ACB)
             for h in range(H):
                 m = slice(h * N, (h + 1) * N)
                 nc.tensor.matmul_mx(
-                    out=acc2[s, j][:],
-                    lhsT=codes[h][:, c].bitcast(E4M3),
-                    lhsT_scale=scales[h][:, c],
+                    out=acc2[s, "u"][:],
+                    lhsT=use_codes[h][:].bitcast(E4M3),
+                    lhsT_scale=use_scales[h][:],
                     rhs=h_codes[s][:, m].bitcast(E5M2),
                     rhs_scale=h_scales[s][:, m],
                     start=(h == 0),
                     stop=(h == H - 1),
                 )
 
-        def cp2(s, j):
-            into = rel if j == "u" else best
-            into[s] = work.tile([P, N], F32, name="rel" if j == "u" else "best", bufs=2)
-            nc.scalar.copy(out=into[s][:], in_=acc2[s, j][:])
+        def ucp(s):
+            rel_t[s] = work.tile([P, N], F32, name="rel_t", bufs=2)
+            nc.scalar.copy(out=rel_t[s][:], in_=acc2[s, "u"][:])
 
-        def mxx(s, j, c0, c1):
-            d = best[s][:, c0:c1]
-            nc.vector.tensor_tensor(out=d, in0=acc2[s, j][:, c0:c1], in1=d, op=ALU.max)
+        def utr(s):
+            rel[s] = psum.tile([P, N], F32, name="tr", bufs=TRB)
+            for r in range(R):
+                c = slice(128 * r, 128 * r + 128)
+                nc.tensor.transpose(rel[s][:, c], rel_t[s][:, c], ident[:])
 
-        def fin(s, c0, c1):
-            if s not in res_t:
-                res_t[s] = work.tile([P, N], F32, name="res_t", bufs=2)
-            nc.vector.scalar_tensor_tensor(
-                out=res_t[s][:, c0:c1], in0=best[s][:, c0:c1], scalar=nlam[:], in1=rel[s][:, c0:c1], op0=ALU.mult, op1=ALU.add
+        def mx2(s, r, k):
+            acc2[s, r, k] = psum.tile([P, N], F32, name="acc", bufs=ACB)
+            for h in range(H):
+                m = slice(h * N + 128 * r, h * N + 128 * r + 128)
+                c = slice(512 * k, 512 * k + 512)
+                nc.tensor.matmul_mx(
+                    out=acc2[s, r, k][:],
+                    lhsT=h_codes[s][:, m].bitcast(E5M2),
+                    lhsT_scale=h_scales[s][:, m],
+                    rhs=sel_codes[h][:, c].bitcast(E4M3),
+                    rhs_scale=sel_scales[h][:, c],
+                    start=(h == 0),
+                    stop=(h == H - 1),
+                )
+
+        def mxr(s, r, k):
+            nc.vector.tensor_reduce(
+                out=red[s][:, r, 32 * k : 32 * k + 32],
+                in_=acc2[s, r, k][:].rearrange("p (u j) -> p u j", j=SLATE),
+                op=ALU.max,
+                axis=AXES.X,
             )
 
         out_view = out.rearrange("(s p r) u -> s p r u", s=SLABS, r=R)
-        o_bank = {}
 
-        def otr(s, r0, r1):
-            o_bank[s, r0] = psum.tile([P, N], F32, name="tr", bufs=TRB)
-            for r in range(r0, r1):
-                nc.tensor.transpose(o_bank[s, r0][:, 128 * (r - r0) : 128 * (r - r0) + 128], res_t[s][:, 128 * r : 128 * r + 128], ident[:])
+        def lm(s, r, u0, u1):
+            d = red[s][:, r, u0:u1]
+            nc.vector.tensor_tensor(out=d, in0=d, in1=lam_row[:, u0:u1], op=ALU.mult)
 
-        def oc(s, r0, r1, e):
-            res = work.tile([P, r1 - r0, USERS], F32, name="res%d" % (r1 - r0), bufs=2)
-            d, i = res[:].rearrange("p r u -> p (r u)"), o_bank[s, r0][:, : 128 * (r1 - r0)]
-            if e == "v":
-                nc.vector.tensor_copy(out=d, in_=i)
-            else:
-                nc.scalar.copy(out=d, in_=i)
-            nc.sync.dma_start(out=out_view[s][:, r0:r1], in_=res[:])
+        def lmg(s, r, u0, u1):
+            d = red[s][:, r, u0:u1]
+            nc.gpsimd.tensor_tensor(out=d, in0=d, in1=lam_row[:, u0:u1], op=ALU.mult)
+
+        def fin(s, r, u0, u1):
+            nc.vector.tensor_tensor(
+                out=res[s][:, r, u0:u1], in0=rel[s][:, 128 * r + u0 : 128 * r + u1], in1=red[s][:, r, u0:u1], op=ALU.subtract
+            )
+
+        def st(s, r0, r1):
+            nc.sync.dma_start(out=out_view[s][:, r0:r1], in_=res[s][:, r0:r1])
 
         def btr():
             x_bank["b"] = psum.tile([P, P], BF16, name="tr", bufs=TRB)
@@ -288,10 +312,21 @@ def tile_marginal_relevance_slates_s9_kernel(tc, x, w_words, w_scales, b, users,
 
         def bcopy():
             nc.vector.tensor_copy(out=bias[:, 0:9], in_=x_bank["b"][:, 0:9])
-            nc.vector.tensor_scalar(out=nlam[:], in0=x_bank["b"][:, 8:9], scalar1=-1.0, scalar2=None, op0=ALU.mult)
+
+        def ltr():
+            x_bank["l"] = psum.tile([P, P], F32, name="tr", bufs=TRB)
+            nc.tensor.matmul(x_bank["l"][:], lhsT=bias[:, 8:9].to_broadcast([P, P]), rhs=ident[:], start=True, stop=True)
+
+        def lcopy():
+            nc.scalar.copy(out=lam_row[:], in_=x_bank["l"][:])
+
+        def dm(n, key):
+            bank = psum.tile([P, N], F32, name="tr", bufs=TRB)
+            for i in range(n):
+                nc.tensor.matmul(bank[:], lhsT=zero[:, 0:128], rhs=zero[:], start=True, stop=True)
 
 
-        pe, act, dve, pool = [], [], [], []
+        pe, act, dve, pool, sp = [], [], [], [], []
         TRB, ACB = 4, 4
 
         def relus(s, h, t0):
@@ -300,76 +335,59 @@ def tile_marginal_relevance_slates_s9_kernel(tc, x, w_words, w_scales, b, users,
         def pair(s, h, t0):
             return [("mx1", s, h, t, g) for t in (t0, t0 + 1) for g in range(G)]
 
-        def trs(s, gp):
-            return [("tr", s, g, rp) for rp in range(2) for g in (2 * gp, 2 * gp + 1)]
+        def trs(s, gp, rp):
+            return [("tr", s, g, rp) for g in (2 * gp, 2 * gp + 1)]
 
-        pe += trs(0, 0) + trs(0, 1) + [("btr",)]
+        pe += [("dm", 7, 0)]
+        pe += trs(0, 0, 0) + trs(0, 0, 1) + [("dm", 2, 1)] + trs(0, 1, 0) + trs(0, 1, 1) + [("btr",)]
         pe += [("mx1", 0, 0, t, g) for g in range(G) for t in (0, 1)]
+        pe += [("ltr",)]
         pe += pair(0, 0, 2) + pair(0, 1, 0)
-        pe += trs(1, 0) + pair(0, 1, 2) + trs(1, 1)
+        pe += trs(1, 0, 0) + trs(1, 0, 1) + pair(0, 1, 2) + trs(1, 1, 0) + trs(1, 1, 1)
         pe += [("mx1", 1, 0, t, g) for g in range(G) for t in (0, 1)]
-        seq = [0, 1, 2, 3, "u"] + list(range(4, 16))
-        EARLY = [0, 2, 3, 3]
-        LEAD = 8
-        pe += [("mx2", 0, j) for j in seq[0:0]]
-        pe += pair(1, 0, 2) + [("mx2", 0, j) for j in seq[0:2]]
-        pe += pair(1, 1, 0) + [("mx2", 0, j) for j in seq[2:5]]
-        pe += pair(1, 1, 2)
-        two = [(0, j) for j in seq[:5]]
-        rest = []
-        for i in range(5, 17 + LEAD):
-            if i < 17:
-                rest.append((0, seq[i]))
-            if i >= LEAD:
-                rest.append((1, seq[i - LEAD]))
-        two += rest
-        for i, n in enumerate(rest):
-            pe += [("mx2",) + n] + ([("otr", 0, 0, 4)] if i == len(rest) - 3 else [])
-        pe += [("otr", 1, 0, 2), ("otr", 1, 2, 4)]
+        A = [("mx2", 0, r, k) for k in range(4) for r in range(4)]
+        B = [("mx2", 1, r, k) for r in range(4) for k in range(4)]
+        pe += pair(1, 0, 2) + A[0:3] + pair(1, 1, 0) + A[3:6] + pair(1, 1, 2)
+        pe += A[6:16] + [("mxu", 0), ("mxu", 1)] + B[0:4] + [("utr", 0)] + B[4:8] + [("utr", 1)] + B[8:]
 
-        act += [("xc", 0, 2 * gp, rp, "s") for gp in range(2) for rp in range(2)]
-        act += [("si", 0, 0, 0, "s")] + relus(0, 0, 0)
+        act += [("xc", 0, 2 * gp + g, rp, "s") for gp in range(2) for rp in range(2) for g in range(2)]
+        act += [("si", 0, 0, 0, "s")] + relus(0, 0, 0) + [("lcopy",)]
         act += [("si", 0, 0, 1, "s")] + relus(0, 0, 2)
-        act += [("si", 0, 3, 1, "s")] + relus(0, 1, 0)
+        act += [("si", 0, 3, 0, "s")] + relus(0, 1, 0)
         act += [("xc", 1, 0, 0, "s"), ("xc", 1, 1, 0, "s"), ("xc", 1, 0, 1, "s")] + relus(0, 1, 2)
-        act += [("xc", 1, 2, 0, "s"), ("xc", 1, 3, 0, "s"), ("xc", 1, 2, 1, "s"), ("si", 1, 0, 0, "s"), ("si", 1, 0, 1, "s")] + relus(1, 0, 0)
+        act += [("xc", 1, 2, 0, "s"), ("xc", 1, 3, 0, "s"), ("xc", 1, 2, 1, "s"), ("si", 1, 0, 0, "s")] + relus(1, 0, 0)
         act += [("si", 1, 1, 0, "s")] + relus(1, 0, 2)
-        act += [("cp2", 0, 0), ("si", 1, 1, 1, "s")] + relus(1, 1, 0)
-        act += [("cp2", 0, "u"), ("si", 1, 2, 1, "s")] + relus(1, 1, 2)
-        act += [("si", 1, 3, 0, "s"), ("si", 1, 3, 1, "s"), ("cp2", 1, 0)]
-        act += [("cp2", 1, "u"), ("oc", 0, 0, 4, "s")]
-        act += [("oc", 1, 0, 2, "s"), ("oc", 1, 2, 4, "s")]
+        act += [("si", 1, 1, 1, "s")] + relus(1, 1, 0)
+        act += [("si", 1, 2, 1, "s")] + relus(1, 1, 2)
+        act += [("si", 1, 3, 0, "s"), ("si", 1, 3, 1, "s"), ("ui", 0, "s"), ("ui", 1, "s"), ("ucp", 0), ("ucp", 1)]
 
-        dve += [("xc", 0, 1, 0, "v")]
-        dve += [("xc", 0, 1, 1, "v")]
-        dve += [("wp", 0, t) for t in range(4)] + [("wsp", t) for t in range(4)]
-        dve += [("xq", 0, 0), ("xq", 0, 1), ("xc", 0, 3, 0, "v"), ("xc", 0, 3, 1, "v"), ("bcopy",), ("xq", 0, 2), ("xq", 0, 3)]
-        dve += [("si", 0, 1, 0, "v"), ("si", 0, 2, 0, "v")]
-        dve += [("wp", 1, t) for t in range(4)]
-        dve += [("si", 0, 3, 0, "v"), ("si", 0, 1, 1, "v"), ("si", 0, 2, 1, "v"), ("sq", 0, 1), ("hi", 0, 0), ("sq", 0, 0), ("hq", 0, 0)]
-        dve += [("xc", 1, 1, 1, "v"), ("sq", 0, 2), ("xq", 1, 0), ("xq", 1, 1), ("sq", 0, 3)]
-        dve += [("si", 1, 2, 0, "v"), ("xc", 1, 3, 1, "v"), ("xq", 1, 2), ("xq", 1, 3), ("hi", 0, 1)]
-        dve += [("ui", 0), ("hq", 0, 1), ("ui", 1), ("uq", 0), ("uq", 1), ("sq", 1, 0)]
-        mm = {}
-        full = {}
-        HALF = {(0, 2), (0, 3), (0, 4), (0, 5), (0, 6)} | {(1, j) for j in range(8, 16)}
-        for s, j in two:
-            if j not in ("u", 0):
-                mm[s, j] = [("mxx", s, j, 0, 256), ("mxx", s, j, 256, 512)] if (s, j) in HALF else [("mxx", s, j, 0, 512)]
-        dve += mm[0, 1] + [("hi", 1, 0), ("sq", 1, 1), ("hq", 1, 0)] + mm[0, 2] + mm[0, 3]
-        dve += [("sq", 1, 2), ("hi", 1, 1)] + mm[0, 4] + [("hq", 1, 1)] + mm[0, 5] + mm[0, 6] + [("sq", 1, 3)]
-        for s, j in rest:
-            if j in ("u", 0) or (s == 0 and j < 7):
-                continue
-            dve += mm[s, j]
-            if (s, j) == (1, 9):
-                dve += [("fin", 0, 0, 512)]
-        dve += [("fin", 1, 0, 256), ("fin", 1, 256, 512)]
+        dve += [("wp", 0), ("wsp",)]
+        dve += [("xq", 0, g) for g in range(4)] + [("bcopy",)]
+        dve += [("si", 0, 1, 0, "v"), ("si", 0, 1, 1, "v"), ("wp", 1)]
+        dve += [("si", 0, 2, 0, "v"), ("si", 0, 2, 1, "v"), ("sq", 0, 1), ("hi", 0, 0), ("sq", 0, 0), ("hq", 0, 0)]
+        dve += [("si", 0, 3, 1, "v"), ("xc", 1, 1, 1, "v"), ("xq", 1, 0), ("xq", 1, 1), ("sq", 0, 2), ("sq", 0, 3)]
+        dve += [("hi", 0, 1), ("xc", 1, 3, 1, "v"), ("xq", 1, 2), ("xq", 1, 3), ("hq", 0, 1), ("si", 1, 0, 1, "v"), ("si", 1, 2, 0, "v"), ("sq", 1, 0)]
+        def reds(items):
+            return [("mxr",) + i[1:] for i in items]
 
-        fns = dict(wp=make_wperm, wsp=make_wsperm, tr=tr, xc=xc, xq=xq, mx1=mx1, relu=relu, hi=hi, hq=hq, si=si, sq=sq, ui=ui, uq=uq, mx2=mx2, cp2=cp2, mxx=mxx, fin=fin, otr=otr, oc=oc, btr=btr, bcopy=bcopy)
+        dve += reds(A[0:1]) + [("sq", 1, 1)] + reds(A[1:2]) + [("hi", 1, 0)] + reds(A[2:3]) + [("hq", 1, 0)]
+        dve += reds(A[3:5]) + [("sq", 1, 2)] + reds(A[5:6]) + [("hi", 1, 1)] + reds(A[6:7]) + [("hq", 1, 1)]
+        dve += reds(A[7:9]) + [("sq", 1, 3)] + reds(A[9:11]) + [("uq", 0), ("uq", 1)] + reds(A[11:16])
+        dve += reds(B[0:5])
+        for r in range(4):
+            pool += [("lmg", 0, r, 0, 128)]
+            dve += [("mxr",) + B[5 + r][1:], ("fin", 0, r, 0, 128)]
+        sp += [("st", 0, 0, 4)]
+        pool += [("lmg", 1, 0, 0, 128), ("lmg", 1, 1, 0, 128)]
+        dve += [("mxr",) + B[i][1:] for i in range(9, 11)] + [("fin", 1, 0, 0, 128), ("mxr",) + B[11][1:], ("fin", 1, 1, 0, 128), ("mxr",) + B[12][1:]]
+        sp += [("st", 1, 0, 2)]
+        dve += [("lm", 1, 2, 0, 128), ("mxr",) + B[13][1:], ("fin", 1, 2, 0, 128), ("mxr",) + B[14][1:], ("lm", 1, 3, 0, 96), ("mxr",) + B[15][1:], ("fin", 1, 3, 0, 96), ("lm", 1, 3, 96, 128), ("fin", 1, 3, 96, 128)]
+        sp += [("st", 1, 2, 3), ("st", 1, 3, 4)]
+
+        fns = dict(wp=wp, wsp=wsp, tr=tr, xc=xc, xq=xq, mx1=mx1, relu=relu, hi=hi, hq=hq, si=si, sq=sq, ui=ui, uq=uq, mxu=mxu, ucp=ucp, utr=utr, mx2=mx2, mxr=mxr, lm=lm, lmg=lmg, fin=fin, st=st, btr=btr, bcopy=bcopy, ltr=ltr, lcopy=lcopy, dm=dm)
 
         def strip(n):
-            return n[:-1] if n[0] in ("xc", "si", "oc") else n
+            return n[:-1] if n[0] in ("xc", "si", "ui") else n
 
         tr_ring, acc_ring = [], []
         for n in pe:
@@ -377,12 +395,18 @@ def tile_marginal_relevance_slates_s9_kernel(tc, x, w_words, w_scales, b, users,
                 tr_ring.append((n, [("xc",) + n[1:]]))
             elif n[0] == "btr":
                 tr_ring.append((n, [("bcopy",)]))
-            elif n[0] == "otr":
-                tr_ring.append((n, [("oc",) + n[1:]]))
+            elif n[0] == "ltr":
+                tr_ring.append((n, [("lcopy",)]))
+            elif n[0] == "dm":
+                tr_ring.append((n, []))
+            elif n[0] == "utr":
+                tr_ring.append((n, [m for m in dve if m[:2] == ("fin", n[1])]))
             elif n[0] == "mx1" and n[4] == 0:
                 acc_ring.append((n, [("relu",) + n[1:4]]))
             elif n[0] == "mx2":
-                acc_ring.append((n, [("cp2",) + n[1:]] if n[2] in ("u", 0) else [m for m in dve if m[:3] == ("mxx", n[1], n[2])]))
+                acc_ring.append((n, [("mxr",) + n[1:]]))
+            elif n[0] == "mxu":
+                acc_ring.append((n, [("ucp",) + n[1:]]))
         ring_need = {}
         for ring, bufs in ((tr_ring, TRB), (acc_ring, ACB)):
             for i in range(bufs, len(ring)):
@@ -396,7 +420,7 @@ def tile_marginal_relevance_slates_s9_kernel(tc, x, w_words, w_scales, b, users,
             elif k == "xq":
                 r += [("xc", n[1], n[2], 0), ("xc", n[1], n[2], 1)]
             elif k == "mx1":
-                r += [("xq", n[1], n[4]), ("wp", n[2], n[3]), ("wsp", n[3])]
+                r += [("xq", n[1], n[4]), ("wp", n[2]), ("wsp",)]
             elif k == "relu":
                 r += [("mx1", n[1], n[2], n[3], 3), ("bcopy",)] + ([("hi", 0, n[2])] if n[1] == 1 else [])
             elif k == "hi":
@@ -407,25 +431,34 @@ def tile_marginal_relevance_slates_s9_kernel(tc, x, w_words, w_scales, b, users,
                 r += [("si", n[1], n[2], 0), ("si", n[1], n[2], 1)]
             elif k == "uq":
                 r += [("ui", n[1])]
+            elif k == "mxu":
+                r += [("hq", n[1], 0), ("hq", n[1], 1), ("uq", 0), ("uq", 1)]
+            elif k == "ucp":
+                r += [("mxu", n[1])]
+            elif k == "utr":
+                r += [("ucp", n[1])]
             elif k == "mx2":
-                r += [("hq", n[1], 0), ("hq", n[1], 1)]
-                r += [("uq", 0), ("uq", 1)] if n[2] == "u" else [("sq", 0, n[2] // 4), ("sq", 1, n[2] // 4)]
-            elif k == "cp2":
-                r += [("mx2", n[1], n[2])]
-            elif k == "mxx":
-                r += [("mx2", n[1], n[2]), ("cp2", n[1], 0)]
+                r += [("hq", n[1], 0), ("hq", n[1], 1), ("sq", 0, n[3]), ("sq", 1, n[3])]
+            elif k == "mxr":
+                r += [("mx2",) + n[1:]]
+            elif k in ("lm", "lmg"):
+                r += [("mxr", n[1], n[2], q) for q in range(n[3] // 32, n[4] // 32)] + [("lcopy",)]
             elif k == "fin":
-                r += [("cp2", n[1], "u")]
-            elif k == "otr":
-                r += [("fin", n[1], 128 * n[2], 128 * n[3])]
-            elif k == "oc":
-                r += [("otr", n[1], n[2], n[3])]
+                lms = [m for m in dve + pool if m[0] in ("lm", "lmg") and m[1:3] == n[1:3] and m[3] <= n[3] and m[4] >= n[4]]
+                assert lms
+                r += lms + [("utr", n[1])]
+            elif k == "st":
+                r += [m for m in dve if m[0] == "fin" and m[1] == n[1] and n[2] <= m[2] < n[3]]
             elif k == "bcopy":
                 r += [("btr",)]
+            elif k == "ltr":
+                r += [("bcopy",)]
+            elif k == "lcopy":
+                r += [("ltr",)]
             return r
 
         done = set()
-        order = [list(pe), list(act), list(dve), list(pool)]
+        order = [list(pe), list(act), list(dve), list(pool), list(sp)]
         while any(order):
             moved = False
             for q in order:

@@ -58,26 +58,30 @@ def tile_marginal_relevance_slates_s9_kernel(tc, x, w_words, w_scales, b, users,
             for q in range(4):
                 nc.sync.dma_start(out=ws_raw_i[32 * q : 32 * q + 4], in_=ws_view[4 * q : 4 * q + 4])
 
-        rows = keep.tile([P, P], BF16, name="rows")
-        sel_view = selected.rearrange("(h b t i) c -> h t b i c", h=H, t=T, i=8)
-        use_view = users.rearrange("(h b t i) c -> h t b i c", h=H, t=T, i=8)
-        sel_raw = [keep.tile([P, T, 2048], BF16, name="sel_raw%d" % h) for h in range(H)]
-        use_raw = [keep.tile([P, T, USERS], BF16, name="use_raw%d" % h) for h in range(H)]
+        b_rows = keep.tile([P, N], BF16, name="b_rows")
+        b_perm = keep.tile([P, T, P], BF16, name="b_perm")
+        lam_rows = keep.tile([P, P], BF16, name="lam_rows")
+        ones = keep.tile([P, P], BF16, name="ones")
+        sel_view = selected.rearrange("(h j t i) c -> h t j i c", h=H, t=T, i=4)
+        use_view = users.rearrange("(h j t i) c -> h t j i c", h=H, t=T, i=4)
+        sel_raw = [[keep.tile([P, T, 1024], BF16, name="sel_raw%d%d" % (h, half)) for half in range(2)] for h in range(H)]
+        use_raw = keep.tile([P, H, T, USERS], BF16, name="use_raw")
 
         def load_selected(h, half):
             c = slice(1024 * half, 1024 * half + 1024)
             for t in range(T):
-                nc.sync.dma_start(out=sel_raw[h][:, t, c], in_=sel_view[h, t][:, :, c])
+                nc.sync.dma_start(out=sel_raw[h][half][:, t, :], in_=sel_view[h, t][:, :, c])
 
         def load_rows():
-            for h in range(H):
-                nc.sync.dma_start(out=rows[4 * h : 4 * h + 4, :].rearrange("t (b i) -> t b i", i=8), in_=b_view[h])
-            nc.sync.dma_start(out=rows[8:9, :], in_=lam.rearrange("(o u) -> o u", o=1))
+            nc.sync.dma_start(out=b_rows[0:H, :], in_=b.rearrange("(h n) -> h n", h=H))
+            nc.sync.dma_start(out=lam_rows[0:1, :], in_=lam.rearrange("(o u) -> o u", o=1))
 
+        nc.vector.memset(b_rows[:], 0.0)
+        nc.vector.memset(lam_rows[:], 0.0)
         nc.vector.memset(ws_raw[:].bitcast(I32), 0)
-        nc.vector.memset(rows[:], 0.0)
+        nc.vector.memset(ones[:], 1.0)
         ident_b = keep.tile([P, P], BF16, name="ident_b")
-        bias = keep.tile([P, 16], F32, name="bias")
+        bias = keep.tile([P, H, T], F32, name="bias")
         lam_row = keep.tile([P, USERS], F32, name="lam_row")
         zero = keep.tile([P, N], BF16, name="zero")
         nc.gpsimd.memset(zero[:], 0.0)
@@ -88,46 +92,36 @@ def tile_marginal_relevance_slates_s9_kernel(tc, x, w_words, w_scales, b, users,
         nc.scalar.activation(out=warm[:], in_=warm[:], func=ACT.Relu)
         nc.vector.tensor_copy(out=ident_b[:], in_=ident[:])
 
-        b_view = b.rearrange("(h b t i) -> h t b i", h=H, t=T, i=8)
-        load_w(0)
-        load_ws()
+        load_rows()
         load_x(0, 0, 0)
         load_x(0, 0, 1)
         load_x(0, 1, 0)
+        load_ws()
         load_x(0, 1, 1)
-        load_rows()
+        load_w(0)
         load_selected(0, 0)
         load_w(1)
-        load_selected(0, 1)
+        load_x(1, 1, 0)
+        load_selected(1, 0)
         load_x(1, 0, 0)
         load_x(1, 0, 1)
-        load_selected(1, 0)
-        load_x(1, 1, 0)
         load_x(1, 1, 1)
         load_selected(1, 1)
+        load_selected(0, 1)
         for h in range(H):
             for t in range(T):
-                nc.sync.dma_start(out=use_raw[h][:, t, :], in_=use_view[h, t])
+                nc.sync.dma_start(out=use_raw[:, h, t, :], in_=use_view[h, t])
 
-        steps = {}
-
-        def step(name, needs):
-            def wrap(fn):
-                steps[name] = (needs, fn)
-
-            return wrap
 
         def wp(h):
-            src = w_raw[:, h, :].bitcast(I32).rearrange("p (g b t w) -> p g t b w", b=16, t=T, w=4)
-            dst = w_perm[:, h, :].bitcast(I32).rearrange("p (g t b w) -> p g t b w", b=16, t=T, w=4)
-            for t in range(T):
-                nc.vector.tensor_copy(out=dst[:, :, t], in_=src[:, :, t])
+            src = w_raw[:, h, :].bitcast(I32).rearrange("p (g j t w) -> p g t j w", j=32, t=T, w=2)
+            dst = w_perm[:, h, :].bitcast(I32).rearrange("p (g t j w) -> p g t j w", j=32, t=T, w=2)
+            nc.vector.tensor_copy(out=dst, in_=src)
 
         def wsp():
-            src = ws_raw[:].bitcast(I32).rearrange("p (q b t w) -> p q t b w", b=16, t=T, w=2)
-            dst = ws_perm[:].bitcast(I32).rearrange("p (q t b w) -> p q t b w", b=16, t=T, w=2)
-            for t in range(T):
-                nc.vector.tensor_copy(out=dst[:, :, t], in_=src[:, :, t])
+            src = ws_raw[:].bitcast(I32).rearrange("p (q j t) -> p q t j", j=32, t=T)
+            dst = ws_perm[:].bitcast(I32).rearrange("p (q t j) -> p q t j", j=32, t=T)
+            nc.vector.tensor_copy(out=dst, in_=src)
 
         x_codes = [keep.tile([P, G * N], U32, name="x_codes%d" % s, align_bytes=64) for s in range(SLABS)]
         x_scales = [keep.tile([P, G * N], U8, name="x_scales%d" % s, align_bytes=64) for s in range(SLABS)]
@@ -145,18 +139,19 @@ def tile_marginal_relevance_slates_s9_kernel(tc, x, w_words, w_scales, b, users,
                     nc.tensor.transpose(bank[:, c0 : c0 + 128], words[:, w0 : w0 + 255 : 2], ident[:])
 
         def xc(s, g, rp, e):
-            if (s, g) not in x_in:
-                x_in[s, g] = work.tile([P, N * T], BF16, name="x_in", align_bytes=64, bufs=4)
-            dst = x_in[s, g][:].bitcast(F32).rearrange("p (r n u) -> p r n u", r=R, u=2)[:, 2 * rp : 2 * rp + 2]
+            if (s, g // 2) not in x_in:
+                x_in[s, g // 2] = work.tile([P, 2, N * T], BF16, name="x_in", align_bytes=64, bufs=4)
+            dst = x_in[s, g // 2][:, g % 2].bitcast(F32).rearrange("p (r n u) -> p r n u", r=R, u=2)[:, 2 * rp : 2 * rp + 2]
             src = x_bank[s, g, rp][:].rearrange("p (r u n) -> p r n u", r=2, u=2)
             if e == "v":
                 nc.vector.tensor_copy(out=dst, in_=src)
             else:
                 nc.scalar.copy(out=dst, in_=src)
 
-        def xq(s, g):
-            c = slice(g * N, (g + 1) * N)
-            nc.vector.quantize_mx(out=x_codes[s][:, c].bitcast(E4M3), scales=x_scales[s][:, c], in_=x_in[s, g][:])
+        def xq(s, g, ng):
+            c = slice(g * N, (g + ng) * N)
+            src = x_in[s, g // 2][:, g % 2 : g % 2 + ng].rearrange("p g k -> p (g k)")
+            nc.vector.quantize_mx(out=x_codes[s][:, c].bitcast(E4M3), scales=x_scales[s][:, c], in_=src)
 
         acc1 = {}
         h_raw = {}
@@ -180,17 +175,22 @@ def tile_marginal_relevance_slates_s9_kernel(tc, x, w_words, w_scales, b, users,
 
         def relu(s, h, t):
             if (s, h) not in h_raw:
-                h_raw[s, h] = work.tile([P, T, N], BF16, name="h_raw", bufs=2)
+                h_raw[s, h] = work.tile([P, 2, N, 2], BF16, name="h_raw", bufs=2)
             nc.scalar.activation(
-                out=h_raw[s, h][:, t, :], in_=acc1[s, h, t][:], func=ACT.Relu, bias=bias[:, h * T + t : h * T + t + 1], scale=1.0
+                out=h_raw[s, h][:, t // 2, :, t % 2], in_=acc1[s, h, t][:], func=ACT.Relu, bias=bias[:, h, t : t + 1], scale=1.0
             )
 
         h_codes = [keep.tile([P, H * N], U32, name="h_codes%d" % s, align_bytes=64) for s in range(SLABS)]
         h_scales = [keep.tile([P, H * N], U8, name="h_scales%d" % s, align_bytes=64) for s in range(SLABS)]
 
-        def hi(s, h):
+        def hi(s, h, e):
             h_in[s, h] = work.tile([P, N, T], BF16, name="h_in", align_bytes=64, bufs=2)
-            nc.vector.tensor_copy(out=h_in[s, h][:], in_=h_raw[s, h][:].rearrange("p t n -> p n t"))
+            words = h_raw[s, h][:].rearrange("p a n e -> p (a n e)").bitcast(F32).rearrange("p (a n) -> p n a", a=2)
+            dst = h_in[s, h][:].rearrange("p n t -> p (n t)").bitcast(F32).rearrange("p (n a) -> p n a", a=2)
+            if e == "v":
+                nc.vector.tensor_copy(out=dst, in_=words)
+            else:
+                nc.scalar.copy(out=dst, in_=words)
 
         def hq(s, h):
             c = slice(h * N, (h + 1) * N)
@@ -200,46 +200,46 @@ def tile_marginal_relevance_slates_s9_kernel(tc, x, w_words, w_scales, b, users,
 
         sel_codes = [keep.tile([P, SLATE * USERS], U32, name="sel_codes%d" % h, align_bytes=64) for h in range(H)]
         sel_scales = [keep.tile([P, SLATE * USERS], U8, name="sel_scales%d" % h, align_bytes=64) for h in range(H)]
-        use_codes = [keep.tile([P, USERS], U32, name="use_codes%d" % h, align_bytes=64) for h in range(H)]
-        use_scales = [keep.tile([P, USERS], U8, name="use_scales%d" % h, align_bytes=64) for h in range(H)]
+        use_codes = keep.tile([P, H * USERS], U32, name="use_codes", align_bytes=64)
+        use_scales = keep.tile([P, H * USERS], U8, name="use_scales", align_bytes=64)
         s_in = {}
 
-        def si(h, k, half, e):
-            if (h, k) not in s_in:
-                s_in[h, k] = work.tile([P, N, T], BF16, name="s_in", align_bytes=64, bufs=8)
-            dst = s_in[h, k][:, 256 * half : 256 * half + 256]
-            src = sel_raw[h][:, :, 512 * k + 256 * half : 512 * k + 256 * half + 256].rearrange("p t c -> p c t")
+        def si(h, k, part, parts, e):
+            if (h, k // 2) not in s_in:
+                s_in[h, k // 2] = work.tile([P, 2, N, T], BF16, name="s_in", align_bytes=64, bufs=4)
+            w = N // parts
+            dst = s_in[h, k // 2][:, k % 2, w * part : w * part + w].rearrange("p (c i) t -> p c t i", i=4)
+            c0 = N * (k % 2) + w * part
+            src = sel_raw[h][k // 2][:, :, c0 : c0 + w].rearrange("p t (c i) -> p c t i", i=4)
             if e == "v":
                 nc.vector.tensor_copy(out=dst, in_=src)
             else:
                 nc.scalar.copy(out=dst, in_=src)
 
-        def sq(h, k):
-            c = slice(512 * k, 512 * k + 512)
-            nc.vector.quantize_mx(
-                out=sel_codes[h][:, c].bitcast(E4M3), scales=sel_scales[h][:, c], in_=s_in[h, k][:].rearrange("p c t -> p (c t)")
-            )
+        def sq(h, k, nk):
+            c = slice(N * k, N * k + N * nk)
+            src = s_in[h, k // 2][:, k % 2 : k % 2 + nk].rearrange("p k c t -> p (k c t)")
+            nc.vector.quantize_mx(out=sel_codes[h][:, c].bitcast(E4M3), scales=sel_scales[h][:, c], in_=src)
 
         u_in = {}
 
-        def ui(h, e):
-            u_in[h] = work.tile([P, USERS, T], BF16, name="u_in", align_bytes=64, bufs=2)
-            src = use_raw[h][:].rearrange("p t u -> p u t")
+        def ui(e):
+            u_in[0] = work.tile([P, H, USERS, T], BF16, name="u_in", align_bytes=64, bufs=1)
+            src = use_raw[:].rearrange("p h t u -> p h u t")
             if e == "v":
-                nc.vector.tensor_copy(out=u_in[h][:], in_=src)
+                nc.vector.tensor_copy(out=u_in[0][:], in_=src)
             else:
-                nc.scalar.copy(out=u_in[h][:], in_=src)
+                nc.scalar.copy(out=u_in[0][:], in_=src)
 
-        def uq(h):
+        def uq():
             nc.vector.quantize_mx(
-                out=use_codes[h][:].bitcast(E4M3), scales=use_scales[h][:], in_=u_in[h][:].rearrange("p u t -> p (u t)")
+                out=use_codes[:].bitcast(E4M3), scales=use_scales[:], in_=u_in[0][:].rearrange("p h u t -> p (h u t)")
             )
 
         acc2 = {}
         rel_t = {}
         rel = {}
         red = [keep.tile([P, R, USERS], F32, name="red%d" % s) for s in range(SLABS)]
-        res = [keep.tile([P, R, USERS], F32, name="res%d" % s) for s in range(SLABS)]
 
         def mxu(s):
             acc2[s, "u"] = psum.tile([P, N], F32, name="acc", bufs=ACB)
@@ -247,8 +247,8 @@ def tile_marginal_relevance_slates_s9_kernel(tc, x, w_words, w_scales, b, users,
                 m = slice(h * N, (h + 1) * N)
                 nc.tensor.matmul_mx(
                     out=acc2[s, "u"][:],
-                    lhsT=use_codes[h][:].bitcast(E4M3),
-                    lhsT_scale=use_scales[h][:],
+                    lhsT=use_codes[:, USERS * h : USERS * h + USERS].bitcast(E4M3),
+                    lhsT_scale=use_scales[:, USERS * h : USERS * h + USERS],
                     rhs=h_codes[s][:, m].bitcast(E5M2),
                     rhs_scale=h_scales[s][:, m],
                     start=(h == 0),
@@ -290,32 +290,42 @@ def tile_marginal_relevance_slates_s9_kernel(tc, x, w_words, w_scales, b, users,
 
         out_view = out.rearrange("(s p r) u -> s p r u", s=SLABS, r=R)
 
-        def lm(s, r, u0, u1):
-            d = red[s][:, r, u0:u1]
-            nc.vector.tensor_tensor(out=d, in0=d, in1=lam_row[:, u0:u1], op=ALU.mult)
+        def lam_view(r0, r1, u0, u1):
+            return lam_row[:, u0:u1].unsqueeze(1).to_broadcast([P, r1 - r0, u1 - u0])
 
-        def lmg(s, r, u0, u1):
-            d = red[s][:, r, u0:u1]
-            nc.gpsimd.tensor_tensor(out=d, in0=d, in1=lam_row[:, u0:u1], op=ALU.mult)
+        def lm(s, r0, r1, u0, u1, e):
+            d = red[s][:, r0:r1, u0:u1]
+            eng = nc.vector if e == "v" else nc.gpsimd
+            eng.tensor_tensor(out=d, in0=d, in1=lam_view(r0, r1, u0, u1), op=ALU.mult)
 
-        def fin(s, r, u0, u1):
+        def fin(s, r0, r1, u0, u1):
             nc.vector.tensor_tensor(
-                out=res[s][:, r, u0:u1], in0=rel[s][:, 128 * r + u0 : 128 * r + u1], in1=red[s][:, r, u0:u1], op=ALU.subtract
+                out=red[s][:, r0:r1, u0:u1],
+                in0=rel[s][:].rearrange("p (r u) -> p r u", r=R)[:, r0:r1, u0:u1],
+                in1=red[s][:, r0:r1, u0:u1],
+                op=ALU.subtract,
             )
 
         def st(s, r0, r1):
-            nc.sync.dma_start(out=out_view[s][:, r0:r1], in_=res[s][:, r0:r1])
+            nc.sync.dma_start(out=out_view[s][:, r0:r1], in_=red[s][:, r0:r1])
+
+        def bperm():
+            nc.scalar.copy(
+                out=b_perm[:].rearrange("p t (j i) -> p t j i", i=4),
+                in_=b_rows[:].rearrange("p (j t i) -> p t j i", t=T, i=4),
+            )
 
         def btr():
-            x_bank["b"] = psum.tile([P, P], BF16, name="tr", bufs=TRB)
-            nc.tensor.transpose(x_bank["b"][:], rows[:], ident_b[:])
+            x_bank["b"] = psum.tile([P, T, P], BF16, name="tr", bufs=TRB)
+            for t in range(T):
+                nc.tensor.transpose(x_bank["b"][:, t, :], b_perm[:, t, :], ident_b[:])
 
         def bcopy():
-            nc.vector.tensor_copy(out=bias[:, 0:9], in_=x_bank["b"][:, 0:9])
+            nc.vector.tensor_copy(out=bias[:], in_=x_bank["b"][:, :, 0:H].rearrange("p t h -> p h t"))
 
         def ltr():
             x_bank["l"] = psum.tile([P, P], F32, name="tr", bufs=TRB)
-            nc.tensor.matmul(x_bank["l"][:], lhsT=bias[:, 8:9].to_broadcast([P, P]), rhs=ident[:], start=True, stop=True)
+            nc.tensor.matmul(x_bank["l"][:], lhsT=ones[:], rhs=lam_rows[:], start=True, stop=True)
 
         def lcopy():
             nc.scalar.copy(out=lam_row[:], in_=x_bank["l"][:])
@@ -325,69 +335,17 @@ def tile_marginal_relevance_slates_s9_kernel(tc, x, w_words, w_scales, b, users,
             for i in range(n):
                 nc.tensor.matmul(bank[:], lhsT=zero[:, 0:128], rhs=zero[:], start=True, stop=True)
 
-
-        pe, act, dve, pool, sp = [], [], [], [], []
         TRB, ACB = 4, 4
+        pe = [('dm', 7, 0), ('ltr',), ('btr',), ('tr', 0, 0, 0), ('tr', 0, 1, 0), ('tr', 0, 1, 1), ('tr', 0, 0, 1), ('dm', 2, 1), ('tr', 0, 2, 0), ('tr', 0, 3, 0), ('tr', 0, 2, 1), ('tr', 0, 3, 1), ('dm', 4, 2), ('mx1', 0, 0, 3, 0), ('mx1', 0, 0, 3, 1), ('mx1', 0, 0, 2, 0), ('mx1', 0, 0, 2, 1), ('mx1', 0, 0, 0, 0), ('mx1', 0, 0, 0, 1), ('mx1', 0, 0, 0, 2), ('mx1', 0, 0, 0, 3), ('mx1', 0, 0, 3, 2), ('mx1', 0, 0, 3, 3), ('mx1', 0, 0, 2, 2), ('mx1', 0, 0, 2, 3), ('mx1', 0, 0, 1, 0), ('mx1', 0, 0, 1, 1), ('mx1', 0, 0, 1, 2), ('mx1', 0, 0, 1, 3), ('tr', 1, 3, 0), ('tr', 1, 2, 0), ('mx1', 0, 1, 3, 0), ('mx1', 0, 1, 3, 1), ('mx1', 0, 1, 0, 0), ('mx1', 0, 1, 0, 1), ('mx1', 0, 1, 0, 2), ('mx1', 0, 1, 0, 3), ('mx1', 0, 1, 3, 2), ('mx1', 0, 1, 3, 3), ('tr', 1, 1, 0), ('tr', 1, 0, 0), ('tr', 1, 1, 1), ('tr', 1, 0, 1), ('mx1', 0, 1, 2, 0), ('mx1', 0, 1, 2, 1), ('tr', 1, 3, 1), ('tr', 1, 2, 1), ('mx1', 0, 1, 2, 2), ('mx1', 0, 1, 2, 3), ('mx1', 0, 1, 1, 0), ('mx1', 0, 1, 1, 1), ('mx1', 0, 1, 1, 2), ('mx1', 0, 1, 1, 3), ('mx1', 1, 1, 0, 0), ('mx1', 1, 1, 0, 1), ('mx1', 1, 1, 2, 0), ('mx1', 1, 1, 2, 1), ('mx1', 1, 1, 2, 2), ('mx1', 1, 1, 2, 3), ('mx1', 1, 1, 3, 0), ('mx1', 1, 1, 3, 1), ('mx1', 1, 1, 3, 2), ('mx1', 1, 1, 3, 3), ('mx1', 1, 1, 0, 2), ('mx1', 1, 1, 0, 3), ('mx1', 1, 1, 1, 0), ('mx1', 1, 1, 1, 1), ('mx1', 1, 1, 1, 2), ('mx1', 1, 1, 1, 3), ('mx2', 0, 3, 1), ('mx1', 1, 0, 0, 0), ('mx1', 1, 0, 0, 1), ('mx2', 0, 3, 0), ('mx1', 1, 0, 3, 0), ('mx1', 1, 0, 3, 1), ('mx1', 1, 0, 0, 2), ('mx1', 1, 0, 0, 3), ('mx1', 1, 0, 3, 2), ('mx1', 1, 0, 3, 3), ('mx1', 1, 0, 1, 0), ('mx1', 1, 0, 1, 1), ('mx1', 1, 0, 1, 2), ('mx1', 1, 0, 1, 3), ('mx2', 0, 2, 1), ('mx2', 0, 2, 2), ('mx2', 0, 0, 2), ('mx2', 0, 0, 3), ('mx2', 0, 1, 3), ('mx2', 0, 1, 2), ('mx2', 0, 3, 3), ('mx2', 0, 2, 3), ('mx2', 0, 3, 2), ('mx2', 0, 1, 0), ('mx1', 1, 0, 2, 0), ('mx1', 1, 0, 2, 1), ('mx1', 1, 0, 2, 2), ('mx1', 1, 0, 2, 3), ('mx2', 0, 0, 0), ('mx2', 0, 2, 0), ('mxu', 0), ('mx2', 0, 0, 1), ('mx2', 0, 1, 1), ('utr', 0), ('mx2', 1, 2, 3), ('mx2', 1, 3, 3), ('mx2', 1, 3, 2), ('mx2', 1, 2, 2), ('mxu', 1), ('mx2', 1, 2, 1), ('mx2', 1, 1, 0), ('utr', 1), ('mx2', 1, 0, 3), ('mx2', 1, 3, 0), ('mx2', 1, 1, 3), ('mx2', 1, 1, 2), ('mx2', 1, 0, 0), ('mx2', 1, 0, 1), ('mx2', 1, 1, 1), ('mx2', 1, 0, 2), ('mx2', 1, 3, 1), ('mx2', 1, 2, 0)]
+        act = [('bperm',), ('lcopy',), ('xc', 0, 0, 1, 's'), ('xc', 0, 2, 0, 's'), ('xc', 0, 2, 1, 's'), ('xc', 0, 3, 1, 's'), ('si', 0, 1, 0, 2, 's'), ('relu', 0, 0, 0), ('relu', 0, 0, 2), ('relu', 0, 0, 3), ('relu', 0, 0, 1), ('xc', 1, 2, 0, 's'), ('si', 1, 1, 1, 2, 's'), ('relu', 0, 1, 0), ('xc', 1, 1, 0, 's'), ('xc', 1, 0, 0, 's'), ('xc', 1, 1, 1, 's'), ('relu', 0, 1, 3), ('xc', 1, 3, 1, 's'), ('xc', 1, 2, 1, 's'), ('relu', 0, 1, 2), ('relu', 0, 1, 1), ('hi', 0, 1, 's'), ('relu', 1, 1, 2), ('relu', 1, 1, 3), ('relu', 1, 1, 0), ('relu', 1, 1, 1), ('si', 0, 3, 1, 2, 's'), ('si', 0, 2, 1, 2, 's'), ('relu', 1, 0, 0), ('relu', 1, 0, 3), ('relu', 1, 0, 1), ('ui', 's'), ('relu', 1, 0, 2), ('hi', 1, 0, 's'), ('ucp', 0), ('ucp', 1)]
+        dve = [('bcopy',), ('xc', 0, 0, 0, 'v'), ('xc', 0, 1, 0, 'v'), ('xc', 0, 1, 1, 'v'), ('wsp',), ('xq', 0, 0, 2), ('xc', 0, 3, 0, 'v'), ('wp', 0), ('xq', 0, 2, 2), ('si', 0, 0, 1, 2, 'v'), ('si', 0, 0, 0, 2, 'v'), ('si', 0, 1, 1, 2, 'v'), ('wp', 1), ('sq', 0, 0, 2), ('xc', 1, 3, 0, 'v'), ('hi', 0, 0, 'v'), ('si', 1, 1, 0, 2, 'v'), ('hq', 0, 0), ('si', 1, 0, 1, 2, 'v'), ('si', 1, 0, 0, 2, 'v'), ('sq', 1, 0, 2), ('xc', 1, 0, 1, 'v'), ('xq', 1, 0, 2), ('xq', 1, 2, 2), ('si', 1, 2, 0, 2, 'v'), ('si', 1, 2, 1, 2, 'v'), ('si', 1, 3, 0, 2, 'v'), ('hq', 0, 1), ('si', 0, 3, 0, 2, 'v'), ('si', 1, 3, 1, 2, 'v'), ('si', 0, 2, 0, 2, 'v'), ('sq', 1, 2, 2), ('hi', 1, 1, 'v'), ('mxr', 0, 3, 1), ('mxr', 0, 3, 0), ('sq', 0, 2, 2), ('hq', 1, 1), ('mxr', 0, 2, 1), ('mxr', 0, 2, 2), ('mxr', 0, 0, 2), ('mxr', 0, 0, 3), ('mxr', 0, 1, 3), ('mxr', 0, 1, 2), ('mxr', 0, 3, 3), ('mxr', 0, 2, 3), ('mxr', 0, 1, 0), ('mxr', 0, 3, 2), ('uq',), ('mxr', 0, 0, 0), ('mxr', 0, 2, 0), ('hq', 1, 0), ('mxr', 0, 0, 1), ('mxr', 0, 1, 1), ('mxr', 1, 2, 3), ('mxr', 1, 3, 3), ('mxr', 1, 3, 2), ('fin', 0, 0, 4, 0, 128), ('mxr', 1, 2, 2), ('mxr', 1, 2, 1), ('mxr', 1, 1, 0), ('mxr', 1, 0, 3), ('mxr', 1, 3, 0), ('mxr', 1, 1, 3), ('mxr', 1, 1, 2), ('mxr', 1, 0, 0), ('mxr', 1, 0, 1), ('mxr', 1, 0, 2), ('mxr', 1, 3, 1), ('mxr', 1, 2, 0), ('mxr', 1, 1, 1), ('lm', 1, 2, 3, 0, 128, 'v'), ('lm', 1, 3, 4, 0, 128, 'v'), ('fin', 1, 2, 3, 0, 128), ('fin', 1, 3, 4, 0, 128), ('fin', 1, 0, 2, 0, 128)]
+        pool = [('lm', 0, 0, 4, 0, 128, 'g'), ('lm', 1, 0, 2, 0, 128, 'g')]
+        sp = [('st', 0, 0, 4), ('st', 1, 0, 2), ('st', 1, 2, 4)]
 
-        def relus(s, h, t0):
-            return [("relu", s, h, t0), ("relu", s, h, t0 + 1)]
-
-        def pair(s, h, t0):
-            return [("mx1", s, h, t, g) for t in (t0, t0 + 1) for g in range(G)]
-
-        def trs(s, gp, rp):
-            return [("tr", s, g, rp) for g in (2 * gp, 2 * gp + 1)]
-
-        pe += [("dm", 7, 0)]
-        pe += trs(0, 0, 0) + trs(0, 0, 1) + [("dm", 2, 1)] + trs(0, 1, 0) + trs(0, 1, 1) + [("btr",)]
-        pe += [("mx1", 0, 0, t, g) for g in range(G) for t in (0, 1)]
-        pe += [("ltr",)]
-        pe += pair(0, 0, 2) + pair(0, 1, 0)
-        pe += trs(1, 0, 0) + trs(1, 0, 1) + pair(0, 1, 2) + trs(1, 1, 0) + trs(1, 1, 1)
-        pe += [("mx1", 1, 0, t, g) for g in range(G) for t in (0, 1)]
-        A = [("mx2", 0, r, k) for k in range(4) for r in range(4)]
-        B = [("mx2", 1, r, k) for r in range(4) for k in range(4)]
-        pe += pair(1, 0, 2) + A[0:3] + pair(1, 1, 0) + A[3:6] + pair(1, 1, 2)
-        pe += A[6:16] + [("mxu", 0), ("mxu", 1)] + B[0:4] + [("utr", 0)] + B[4:8] + [("utr", 1)] + B[8:]
-
-        act += [("xc", 0, 2 * gp + g, rp, "s") for gp in range(2) for rp in range(2) for g in range(2)]
-        act += [("si", 0, 0, 0, "s")] + relus(0, 0, 0) + [("lcopy",)]
-        act += [("si", 0, 0, 1, "s")] + relus(0, 0, 2)
-        act += [("si", 0, 3, 0, "s")] + relus(0, 1, 0)
-        act += [("xc", 1, 0, 0, "s"), ("xc", 1, 1, 0, "s"), ("xc", 1, 0, 1, "s")] + relus(0, 1, 2)
-        act += [("xc", 1, 2, 0, "s"), ("xc", 1, 3, 0, "s"), ("xc", 1, 2, 1, "s"), ("si", 1, 0, 0, "s")] + relus(1, 0, 0)
-        act += [("si", 1, 1, 0, "s")] + relus(1, 0, 2)
-        act += [("si", 1, 1, 1, "s")] + relus(1, 1, 0)
-        act += [("si", 1, 2, 1, "s")] + relus(1, 1, 2)
-        act += [("si", 1, 3, 0, "s"), ("si", 1, 3, 1, "s"), ("ui", 0, "s"), ("ui", 1, "s"), ("ucp", 0), ("ucp", 1)]
-
-        dve += [("wp", 0), ("wsp",)]
-        dve += [("xq", 0, g) for g in range(4)] + [("bcopy",)]
-        dve += [("si", 0, 1, 0, "v"), ("si", 0, 1, 1, "v"), ("wp", 1)]
-        dve += [("si", 0, 2, 0, "v"), ("si", 0, 2, 1, "v"), ("sq", 0, 1), ("hi", 0, 0), ("sq", 0, 0), ("hq", 0, 0)]
-        dve += [("si", 0, 3, 1, "v"), ("xc", 1, 1, 1, "v"), ("xq", 1, 0), ("xq", 1, 1), ("sq", 0, 2), ("sq", 0, 3)]
-        dve += [("hi", 0, 1), ("xc", 1, 3, 1, "v"), ("xq", 1, 2), ("xq", 1, 3), ("hq", 0, 1), ("si", 1, 0, 1, "v"), ("si", 1, 2, 0, "v"), ("sq", 1, 0)]
-        def reds(items):
-            return [("mxr",) + i[1:] for i in items]
-
-        dve += reds(A[0:1]) + [("sq", 1, 1)] + reds(A[1:2]) + [("hi", 1, 0)] + reds(A[2:3]) + [("hq", 1, 0)]
-        dve += reds(A[3:5]) + [("sq", 1, 2)] + reds(A[5:6]) + [("hi", 1, 1)] + reds(A[6:7]) + [("hq", 1, 1)]
-        dve += reds(A[7:9]) + [("sq", 1, 3)] + reds(A[9:11]) + [("uq", 0), ("uq", 1)] + reds(A[11:16])
-        dve += reds(B[0:5])
-        for r in range(4):
-            pool += [("lmg", 0, r, 0, 128)]
-            dve += [("mxr",) + B[5 + r][1:], ("fin", 0, r, 0, 128)]
-        sp += [("st", 0, 0, 4)]
-        pool += [("lmg", 1, 0, 0, 128), ("lmg", 1, 1, 0, 128)]
-        dve += [("mxr",) + B[i][1:] for i in range(9, 11)] + [("fin", 1, 0, 0, 128), ("mxr",) + B[11][1:], ("fin", 1, 1, 0, 128), ("mxr",) + B[12][1:]]
-        sp += [("st", 1, 0, 2)]
-        dve += [("lm", 1, 2, 0, 128), ("mxr",) + B[13][1:], ("fin", 1, 2, 0, 128), ("mxr",) + B[14][1:], ("lm", 1, 3, 0, 96), ("mxr",) + B[15][1:], ("fin", 1, 3, 0, 96), ("lm", 1, 3, 96, 128), ("fin", 1, 3, 96, 128)]
-        sp += [("st", 1, 2, 3), ("st", 1, 3, 4)]
-
-        fns = dict(wp=wp, wsp=wsp, tr=tr, xc=xc, xq=xq, mx1=mx1, relu=relu, hi=hi, hq=hq, si=si, sq=sq, ui=ui, uq=uq, mxu=mxu, ucp=ucp, utr=utr, mx2=mx2, mxr=mxr, lm=lm, lmg=lmg, fin=fin, st=st, btr=btr, bcopy=bcopy, ltr=ltr, lcopy=lcopy, dm=dm)
+        fns = dict(wp=wp, wsp=wsp, tr=tr, xc=xc, xq=xq, mx1=mx1, relu=relu, hi=hi, hq=hq, si=si, sq=sq, ui=ui, uq=uq, mxu=mxu, ucp=ucp, utr=utr, mx2=mx2, mxr=mxr, lm=lm, fin=fin, st=st, bperm=bperm, btr=btr, bcopy=bcopy, ltr=ltr, lcopy=lcopy, dm=dm)
 
         def strip(n):
-            return n[:-1] if n[0] in ("xc", "si", "ui") else n
+            return n[:-1] if n[0] in ("xc", "si", "ui", "lm", "hi") else n
 
         tr_ring, acc_ring = [], []
         for n in pe:
@@ -412,47 +370,53 @@ def tile_marginal_relevance_slates_s9_kernel(tc, x, w_words, w_scales, b, users,
             for i in range(bufs, len(ring)):
                 ring_need[ring[i][0]] = ring[i - bufs][1]
 
+        raw_order = []
+        for n in act:
+            if n[0] == "relu" and n[1:3] not in raw_order:
+                raw_order.append(n[1:3])
+        in_order = [n[1:] for n in dve if n[0] == "hq"]
+
         def needs(n):
             k = n[0]
             r = list(ring_need.get(n, []))
             if k == "xc":
-                r += [("tr",) + n[1:4]] + ([("xq", 0, n[2])] if n[1] == 1 else [])
+                r += [("tr",) + n[1:4]]
             elif k == "xq":
-                r += [("xc", n[1], n[2], 0), ("xc", n[1], n[2], 1)]
+                r += [("xc", n[1], g, rp) for g in range(n[2], n[2] + n[3]) for rp in range(2)]
             elif k == "mx1":
-                r += [("xq", n[1], n[4]), ("wp", n[2]), ("wsp",)]
+                r += [m for m in dve if m[0] == "xq" and m[1] == n[1] and m[2] <= n[4] < m[2] + m[3]] + [("wp", n[2]), ("wsp",)]
             elif k == "relu":
-                r += [("mx1", n[1], n[2], n[3], 3), ("bcopy",)] + ([("hi", 0, n[2])] if n[1] == 1 else [])
+                r += [("mx1", n[1], n[2], n[3], 3), ("bcopy",)] + [("hi",) + m for m in raw_order[: max(0, raw_order.index(n[1:3]) - 1)]]
             elif k == "hi":
-                r += [("relu", n[1], n[2], t) for t in range(T)] + ([("hq", 0, n[2])] if n[1] == 1 else [])
+                r += [("relu", n[1], n[2], t) for t in range(T)] + [("hq",) + m for m in in_order[: max(0, in_order.index(n[1:3]) - 1)]] + [("hi",) + m for m in in_order[: in_order.index(n[1:3])]]
             elif k == "hq":
                 r += [("hi", n[1], n[2])]
             elif k == "sq":
-                r += [("si", n[1], n[2], 0), ("si", n[1], n[2], 1)]
+                r += [m[:-1] for m in act + dve + pool if m[0] == "si" and m[1] == n[1] and n[2] <= m[2] < n[2] + n[3]]
             elif k == "uq":
-                r += [("ui", n[1])]
+                r += [("ui",)]
             elif k == "mxu":
-                r += [("hq", n[1], 0), ("hq", n[1], 1), ("uq", 0), ("uq", 1)]
+                r += [("hq", n[1], 0), ("hq", n[1], 1), ("uq",)]
             elif k == "ucp":
                 r += [("mxu", n[1])]
             elif k == "utr":
                 r += [("ucp", n[1])]
             elif k == "mx2":
-                r += [("hq", n[1], 0), ("hq", n[1], 1), ("sq", 0, n[3]), ("sq", 1, n[3])]
+                r += [("hq", n[1], 0), ("hq", n[1], 1), ] + [m for m in dve if m[0] == "sq" and m[2] <= n[3] < m[2] + m[3]]
             elif k == "mxr":
                 r += [("mx2",) + n[1:]]
-            elif k in ("lm", "lmg"):
-                r += [("mxr", n[1], n[2], q) for q in range(n[3] // 32, n[4] // 32)] + [("lcopy",)]
+            elif k == "lm":
+                r += [("mxr", n[1], a, q) for a in range(n[2], n[3]) for q in range(n[4] // 32, n[5] // 32)] + [("lcopy",)]
             elif k == "fin":
-                lms = [m for m in dve + pool if m[0] in ("lm", "lmg") and m[1:3] == n[1:3] and m[3] <= n[3] and m[4] >= n[4]]
+                lms = [m[:-1] for m in dve + pool if m[0] == "lm" and m[1] == n[1] and m[2] < n[3] and m[3] > n[2] and m[4] < n[5] and m[5] > n[4]]
                 assert lms
                 r += lms + [("utr", n[1])]
             elif k == "st":
-                r += [m for m in dve if m[0] == "fin" and m[1] == n[1] and n[2] <= m[2] < n[3]]
+                r += [m for m in dve if m[0] == "fin" and m[1] == n[1] and m[2] < n[3] and m[3] > n[2]]
             elif k == "bcopy":
                 r += [("btr",)]
-            elif k == "ltr":
-                r += [("bcopy",)]
+            elif k == "btr":
+                r += [("bperm",)]
             elif k == "lcopy":
                 r += [("ltr",)]
             return r

@@ -93,21 +93,21 @@ def tile_marginal_relevance_slates_s9_kernel(tc, x, w_words, w_scales, b, users,
         nc.vector.tensor_copy(out=ident_b[:], in_=ident[:])
 
         load_rows()
-        load_x(0, 0, 0)
         load_x(0, 0, 1)
-        load_x(0, 1, 0)
         load_ws()
+        load_x(0, 1, 0)
         load_x(0, 1, 1)
-        load_w(0)
-        load_selected(0, 0)
-        load_w(1)
+        load_x(0, 0, 0)
+        load_x(1, 1, 1)
         load_x(1, 1, 0)
-        load_selected(1, 0)
+        load_w(1)
+        load_selected(0, 1)
+        load_w(0)
         load_x(1, 0, 0)
         load_x(1, 0, 1)
-        load_x(1, 1, 1)
+        load_selected(1, 0)
         load_selected(1, 1)
-        load_selected(0, 1)
+        load_selected(0, 0)
         for h in range(H):
             for t in range(T):
                 nc.sync.dma_start(out=use_raw[:, h, t, :], in_=use_view[h, t])
@@ -204,13 +204,12 @@ def tile_marginal_relevance_slates_s9_kernel(tc, x, w_words, w_scales, b, users,
         use_scales = keep.tile([P, H * USERS], U8, name="use_scales", align_bytes=64)
         s_in = {}
 
-        def si(h, k, part, parts, e):
-            if (h, k // 2) not in s_in:
-                s_in[h, k // 2] = work.tile([P, 2, N, T], BF16, name="s_in", align_bytes=64, bufs=4)
-            w = N // parts
-            dst = s_in[h, k // 2][:, k % 2, w * part : w * part + w].rearrange("p (c i) t -> p c t i", i=4)
-            c0 = N * (k % 2) + w * part
-            src = sel_raw[h][k // 2][:, :, c0 : c0 + w].rearrange("p t (c i) -> p c t i", i=4)
+        def si(h, half, q0, nq, e):
+            if (h, half) not in s_in:
+                s_in[h, half] = work.tile([P, 1024, T], BF16, name="s_in", align_bytes=64, bufs=4)
+            c = slice(256 * q0, 256 * (q0 + nq))
+            dst = s_in[h, half][:, c].rearrange("p (c i) t -> p c t i", i=4)
+            src = sel_raw[h][half][:, :, c].rearrange("p t (c i) -> p c t i", i=4)
             if e == "v":
                 nc.vector.tensor_copy(out=dst, in_=src)
             else:
@@ -218,7 +217,7 @@ def tile_marginal_relevance_slates_s9_kernel(tc, x, w_words, w_scales, b, users,
 
         def sq(h, k, nk):
             c = slice(N * k, N * k + N * nk)
-            src = s_in[h, k // 2][:, k % 2 : k % 2 + nk].rearrange("p k c t -> p (k c t)")
+            src = s_in[h, k // 2][:, N * (k % 2) : N * (k % 2 + nk)].rearrange("p c t -> p (c t)")
             nc.vector.quantize_mx(out=sel_codes[h][:, c].bitcast(E4M3), scales=sel_scales[h][:, c], in_=src)
 
         u_in = {}
@@ -320,8 +319,12 @@ def tile_marginal_relevance_slates_s9_kernel(tc, x, w_words, w_scales, b, users,
             for t in range(T):
                 nc.tensor.transpose(x_bank["b"][:, t, :], b_perm[:, t, :], ident_b[:])
 
-        def bcopy():
-            nc.vector.tensor_copy(out=bias[:], in_=x_bank["b"][:, :, 0:H].rearrange("p t h -> p h t"))
+        def bcopy(e):
+            src = x_bank["b"][:, :, 0:H].rearrange("p t h -> p h t")
+            if e == "v":
+                nc.vector.tensor_copy(out=bias[:], in_=src)
+            else:
+                nc.scalar.copy(out=bias[:], in_=src)
 
         def ltr():
             x_bank["l"] = psum.tile([P, P], F32, name="tr", bufs=TRB)
@@ -336,16 +339,16 @@ def tile_marginal_relevance_slates_s9_kernel(tc, x, w_words, w_scales, b, users,
                 nc.tensor.matmul(bank[:], lhsT=zero[:, 0:128], rhs=zero[:], start=True, stop=True)
 
         TRB, ACB = 4, 4
-        pe = [('dm', 7, 0), ('ltr',), ('btr',), ('tr', 0, 0, 0), ('tr', 0, 1, 0), ('tr', 0, 1, 1), ('tr', 0, 0, 1), ('dm', 2, 1), ('tr', 0, 2, 0), ('tr', 0, 3, 0), ('tr', 0, 2, 1), ('tr', 0, 3, 1), ('dm', 4, 2), ('mx1', 0, 0, 3, 0), ('mx1', 0, 0, 3, 1), ('mx1', 0, 0, 2, 0), ('mx1', 0, 0, 2, 1), ('mx1', 0, 0, 0, 0), ('mx1', 0, 0, 0, 1), ('mx1', 0, 0, 0, 2), ('mx1', 0, 0, 0, 3), ('mx1', 0, 0, 3, 2), ('mx1', 0, 0, 3, 3), ('mx1', 0, 0, 2, 2), ('mx1', 0, 0, 2, 3), ('mx1', 0, 0, 1, 0), ('mx1', 0, 0, 1, 1), ('mx1', 0, 0, 1, 2), ('mx1', 0, 0, 1, 3), ('tr', 1, 3, 0), ('tr', 1, 2, 0), ('mx1', 0, 1, 3, 0), ('mx1', 0, 1, 3, 1), ('mx1', 0, 1, 0, 0), ('mx1', 0, 1, 0, 1), ('mx1', 0, 1, 0, 2), ('mx1', 0, 1, 0, 3), ('mx1', 0, 1, 3, 2), ('mx1', 0, 1, 3, 3), ('tr', 1, 1, 0), ('tr', 1, 0, 0), ('tr', 1, 1, 1), ('tr', 1, 0, 1), ('mx1', 0, 1, 2, 0), ('mx1', 0, 1, 2, 1), ('tr', 1, 3, 1), ('tr', 1, 2, 1), ('mx1', 0, 1, 2, 2), ('mx1', 0, 1, 2, 3), ('mx1', 0, 1, 1, 0), ('mx1', 0, 1, 1, 1), ('mx1', 0, 1, 1, 2), ('mx1', 0, 1, 1, 3), ('mx1', 1, 1, 0, 0), ('mx1', 1, 1, 0, 1), ('mx1', 1, 1, 2, 0), ('mx1', 1, 1, 2, 1), ('mx1', 1, 1, 2, 2), ('mx1', 1, 1, 2, 3), ('mx1', 1, 1, 3, 0), ('mx1', 1, 1, 3, 1), ('mx1', 1, 1, 3, 2), ('mx1', 1, 1, 3, 3), ('mx1', 1, 1, 0, 2), ('mx1', 1, 1, 0, 3), ('mx1', 1, 1, 1, 0), ('mx1', 1, 1, 1, 1), ('mx1', 1, 1, 1, 2), ('mx1', 1, 1, 1, 3), ('mx2', 0, 3, 1), ('mx1', 1, 0, 0, 0), ('mx1', 1, 0, 0, 1), ('mx2', 0, 3, 0), ('mx1', 1, 0, 3, 0), ('mx1', 1, 0, 3, 1), ('mx1', 1, 0, 0, 2), ('mx1', 1, 0, 0, 3), ('mx1', 1, 0, 3, 2), ('mx1', 1, 0, 3, 3), ('mx1', 1, 0, 1, 0), ('mx1', 1, 0, 1, 1), ('mx1', 1, 0, 1, 2), ('mx1', 1, 0, 1, 3), ('mx2', 0, 2, 1), ('mx2', 0, 2, 2), ('mx2', 0, 0, 2), ('mx2', 0, 0, 3), ('mx2', 0, 1, 3), ('mx2', 0, 1, 2), ('mx2', 0, 3, 3), ('mx2', 0, 2, 3), ('mx2', 0, 3, 2), ('mx2', 0, 1, 0), ('mx1', 1, 0, 2, 0), ('mx1', 1, 0, 2, 1), ('mx1', 1, 0, 2, 2), ('mx1', 1, 0, 2, 3), ('mx2', 0, 0, 0), ('mx2', 0, 2, 0), ('mxu', 0), ('mx2', 0, 0, 1), ('mx2', 0, 1, 1), ('utr', 0), ('mx2', 1, 2, 3), ('mx2', 1, 3, 3), ('mx2', 1, 3, 2), ('mx2', 1, 2, 2), ('mxu', 1), ('mx2', 1, 2, 1), ('mx2', 1, 1, 0), ('utr', 1), ('mx2', 1, 0, 3), ('mx2', 1, 3, 0), ('mx2', 1, 1, 3), ('mx2', 1, 1, 2), ('mx2', 1, 0, 0), ('mx2', 1, 0, 1), ('mx2', 1, 1, 1), ('mx2', 1, 0, 2), ('mx2', 1, 3, 1), ('mx2', 1, 2, 0)]
-        act = [('bperm',), ('lcopy',), ('xc', 0, 0, 1, 's'), ('xc', 0, 2, 0, 's'), ('xc', 0, 2, 1, 's'), ('xc', 0, 3, 1, 's'), ('si', 0, 1, 0, 2, 's'), ('relu', 0, 0, 0), ('relu', 0, 0, 2), ('relu', 0, 0, 3), ('relu', 0, 0, 1), ('xc', 1, 2, 0, 's'), ('si', 1, 1, 1, 2, 's'), ('relu', 0, 1, 0), ('xc', 1, 1, 0, 's'), ('xc', 1, 0, 0, 's'), ('xc', 1, 1, 1, 's'), ('relu', 0, 1, 3), ('xc', 1, 3, 1, 's'), ('xc', 1, 2, 1, 's'), ('relu', 0, 1, 2), ('relu', 0, 1, 1), ('hi', 0, 1, 's'), ('relu', 1, 1, 2), ('relu', 1, 1, 3), ('relu', 1, 1, 0), ('relu', 1, 1, 1), ('si', 0, 3, 1, 2, 's'), ('si', 0, 2, 1, 2, 's'), ('relu', 1, 0, 0), ('relu', 1, 0, 3), ('relu', 1, 0, 1), ('ui', 's'), ('relu', 1, 0, 2), ('hi', 1, 0, 's'), ('ucp', 0), ('ucp', 1)]
-        dve = [('bcopy',), ('xc', 0, 0, 0, 'v'), ('xc', 0, 1, 0, 'v'), ('xc', 0, 1, 1, 'v'), ('wsp',), ('xq', 0, 0, 2), ('xc', 0, 3, 0, 'v'), ('wp', 0), ('xq', 0, 2, 2), ('si', 0, 0, 1, 2, 'v'), ('si', 0, 0, 0, 2, 'v'), ('si', 0, 1, 1, 2, 'v'), ('wp', 1), ('sq', 0, 0, 2), ('xc', 1, 3, 0, 'v'), ('hi', 0, 0, 'v'), ('si', 1, 1, 0, 2, 'v'), ('hq', 0, 0), ('si', 1, 0, 1, 2, 'v'), ('si', 1, 0, 0, 2, 'v'), ('sq', 1, 0, 2), ('xc', 1, 0, 1, 'v'), ('xq', 1, 0, 2), ('xq', 1, 2, 2), ('si', 1, 2, 0, 2, 'v'), ('si', 1, 2, 1, 2, 'v'), ('si', 1, 3, 0, 2, 'v'), ('hq', 0, 1), ('si', 0, 3, 0, 2, 'v'), ('si', 1, 3, 1, 2, 'v'), ('si', 0, 2, 0, 2, 'v'), ('sq', 1, 2, 2), ('hi', 1, 1, 'v'), ('mxr', 0, 3, 1), ('mxr', 0, 3, 0), ('sq', 0, 2, 2), ('hq', 1, 1), ('mxr', 0, 2, 1), ('mxr', 0, 2, 2), ('mxr', 0, 0, 2), ('mxr', 0, 0, 3), ('mxr', 0, 1, 3), ('mxr', 0, 1, 2), ('mxr', 0, 3, 3), ('mxr', 0, 2, 3), ('mxr', 0, 1, 0), ('mxr', 0, 3, 2), ('uq',), ('mxr', 0, 0, 0), ('mxr', 0, 2, 0), ('hq', 1, 0), ('mxr', 0, 0, 1), ('mxr', 0, 1, 1), ('mxr', 1, 2, 3), ('mxr', 1, 3, 3), ('mxr', 1, 3, 2), ('fin', 0, 0, 4, 0, 128), ('mxr', 1, 2, 2), ('mxr', 1, 2, 1), ('mxr', 1, 1, 0), ('mxr', 1, 0, 3), ('mxr', 1, 3, 0), ('mxr', 1, 1, 3), ('mxr', 1, 1, 2), ('mxr', 1, 0, 0), ('mxr', 1, 0, 1), ('mxr', 1, 0, 2), ('mxr', 1, 3, 1), ('mxr', 1, 2, 0), ('mxr', 1, 1, 1), ('lm', 1, 2, 3, 0, 128, 'v'), ('lm', 1, 3, 4, 0, 128, 'v'), ('fin', 1, 2, 3, 0, 128), ('fin', 1, 3, 4, 0, 128), ('fin', 1, 0, 2, 0, 128)]
+        pe = [('dm', 7, 0), ('tr', 0, 1, 1), ('tr', 0, 0, 1), ('tr', 0, 2, 0), ('tr', 0, 3, 0), ('dm', 2, 1), ('tr', 0, 2, 1), ('tr', 0, 3, 1), ('tr', 0, 0, 0), ('tr', 0, 1, 0), ('tr', 1, 2, 1), ('tr', 1, 2, 0), ('tr', 1, 3, 1), ('tr', 1, 3, 0), ('btr',), ('dm', 4, 2), ('mx1', 0, 1, 1, 0), ('mx1', 0, 1, 1, 1), ('mx1', 0, 1, 1, 2), ('mx1', 0, 1, 1, 3), ('mx1', 0, 1, 3, 0), ('mx1', 0, 1, 3, 1), ('mx1', 0, 1, 0, 0), ('mx1', 0, 1, 0, 1), ('mx1', 0, 1, 0, 2), ('mx1', 0, 1, 0, 3), ('mx1', 0, 1, 3, 2), ('mx1', 0, 1, 3, 3), ('mx1', 0, 1, 2, 0), ('mx1', 0, 1, 2, 1), ('mx1', 0, 1, 2, 2), ('mx1', 0, 1, 2, 3), ('mx1', 0, 0, 1, 0), ('mx1', 0, 0, 1, 1), ('tr', 1, 0, 0), ('tr', 1, 1, 0), ('tr', 1, 0, 1), ('tr', 1, 1, 1), ('mx1', 0, 0, 1, 2), ('mx1', 0, 0, 1, 3), ('mx1', 0, 0, 0, 0), ('mx1', 0, 0, 0, 1), ('mx1', 0, 0, 3, 0), ('mx1', 0, 0, 3, 1), ('mx1', 0, 0, 2, 0), ('mx1', 0, 0, 2, 1), ('mx1', 0, 0, 0, 2), ('mx1', 0, 0, 0, 3), ('mx1', 0, 0, 3, 2), ('mx1', 0, 0, 3, 3), ('mx1', 1, 1, 3, 0), ('mx1', 1, 1, 3, 1), ('mx1', 0, 0, 2, 2), ('mx1', 0, 0, 2, 3), ('mx1', 1, 1, 2, 0), ('mx1', 1, 1, 2, 1), ('mx1', 1, 1, 3, 2), ('mx1', 1, 1, 3, 3), ('mx1', 1, 1, 0, 0), ('mx1', 1, 1, 0, 1), ('mx1', 1, 1, 2, 2), ('mx1', 1, 1, 2, 3), ('mx1', 1, 1, 1, 0), ('mx1', 1, 1, 1, 1), ('mx1', 1, 1, 0, 2), ('mx1', 1, 1, 0, 3), ('mx1', 1, 1, 1, 2), ('mx1', 1, 1, 1, 3), ('mx1', 1, 0, 0, 0), ('mx1', 1, 0, 0, 1), ('mx2', 0, 2, 2), ('mx1', 1, 0, 0, 2), ('mx1', 1, 0, 0, 3), ('mx2', 0, 1, 2), ('mx2', 0, 0, 3), ('mx2', 0, 3, 3), ('mx2', 0, 2, 3), ('ltr',), ('mx2', 0, 0, 2), ('mx2', 0, 1, 3), ('mx1', 1, 0, 1, 0), ('mx1', 1, 0, 1, 1), ('mx2', 0, 3, 2), ('mx1', 1, 0, 1, 2), ('mx1', 1, 0, 1, 3), ('mx1', 1, 0, 2, 0), ('mx1', 1, 0, 2, 1), ('mx1', 1, 0, 2, 2), ('mx1', 1, 0, 2, 3), ('mx2', 0, 3, 1), ('mx2', 0, 1, 1), ('mx2', 0, 2, 0), ('mx1', 1, 0, 3, 0), ('mx1', 1, 0, 3, 1), ('mx1', 1, 0, 3, 2), ('mx1', 1, 0, 3, 3), ('mx2', 0, 1, 0), ('mx2', 0, 2, 1), ('mx2', 0, 0, 0), ('mxu', 0), ('mx2', 0, 3, 0), ('mx2', 0, 0, 1), ('mx2', 1, 2, 0), ('mx2', 1, 3, 1), ('mxu', 1), ('mx2', 1, 1, 1), ('mx2', 1, 0, 3), ('mx2', 1, 3, 0), ('mx2', 1, 0, 2), ('mx2', 1, 3, 2), ('mx2', 1, 1, 0), ('mx2', 1, 1, 3), ('mx2', 1, 1, 2), ('mx2', 1, 2, 1), ('utr', 0), ('mx2', 1, 2, 2), ('mx2', 1, 3, 3), ('mx2', 1, 0, 0), ('mx2', 1, 0, 1), ('mx2', 1, 2, 3), ('utr', 1)]
+        act = [('bperm',), ('xc', 0, 0, 0, 's'), ('xc', 0, 1, 0, 's'), ('xc', 1, 2, 1, 's'), ('xc', 1, 2, 0, 's'), ('xc', 1, 3, 0, 's'), ('relu', 0, 1, 1), ('si', 0, 1, 1, 1, 's'), ('relu', 0, 1, 0), ('relu', 0, 1, 3), ('relu', 0, 1, 2), ('xc', 1, 0, 0, 's'), ('xc', 1, 0, 1, 's'), ('xc', 1, 1, 1, 's'), ('relu', 0, 0, 1), ('si', 1, 0, 0, 1, 's'), ('relu', 0, 0, 0), ('relu', 0, 0, 3), ('relu', 0, 0, 2), ('hi', 0, 0, 's'), ('relu', 1, 1, 3), ('relu', 1, 1, 2), ('relu', 1, 1, 0), ('relu', 1, 1, 1), ('relu', 1, 0, 0), ('si', 0, 0, 0, 3, 's'), ('hi', 1, 1, 's'), ('relu', 1, 0, 1), ('relu', 1, 0, 2), ('ui', 's'), ('relu', 1, 0, 3), ('lcopy',), ('hi', 1, 0, 's'), ('ucp', 0), ('ucp', 1)]
+        dve = [('wsp',), ('xc', 0, 1, 1, 'v'), ('xc', 0, 0, 1, 'v'), ('xc', 0, 2, 0, 'v'), ('xc', 0, 3, 0, 'v'), ('xc', 0, 2, 1, 'v'), ('xc', 0, 3, 1, 'v'), ('xq', 0, 2, 2), ('xq', 0, 0, 2), ('wp', 1), ('xc', 1, 3, 1, 'v'), ('bcopy', 'v'), ('xq', 1, 2, 2), ('si', 0, 1, 2, 2, 'v'), ('wp', 0), ('si', 0, 1, 0, 1, 'v'), ('sq', 0, 2, 2), ('hi', 0, 1, 'v'), ('xc', 1, 1, 0, 'v'), ('hq', 0, 1), ('xq', 1, 0, 2), ('si', 1, 0, 1, 3, 'v'), ('si', 1, 1, 0, 4, 'v'), ('hq', 0, 0), ('sq', 1, 2, 2), ('si', 0, 0, 3, 1, 'v'), ('sq', 1, 0, 2), ('mxr', 0, 2, 2), ('mxr', 0, 1, 2), ('mxr', 0, 0, 3), ('mxr', 0, 3, 3), ('mxr', 0, 2, 3), ('mxr', 0, 0, 2), ('mxr', 0, 1, 3), ('sq', 0, 0, 2), ('mxr', 0, 3, 2), ('hq', 1, 1), ('mxr', 0, 3, 1), ('mxr', 0, 1, 1), ('uq',), ('mxr', 0, 2, 0), ('mxr', 0, 1, 0), ('mxr', 0, 2, 1), ('mxr', 0, 0, 0), ('hq', 1, 0), ('mxr', 0, 3, 0), ('mxr', 0, 0, 1), ('mxr', 1, 2, 0), ('mxr', 1, 3, 1), ('mxr', 1, 1, 1), ('mxr', 1, 0, 3), ('mxr', 1, 3, 0), ('mxr', 1, 0, 2), ('mxr', 1, 3, 2), ('mxr', 1, 1, 0), ('mxr', 1, 1, 2), ('mxr', 1, 2, 1), ('mxr', 1, 1, 3), ('fin', 0, 0, 4, 0, 128), ('mxr', 1, 2, 2), ('mxr', 1, 3, 3), ('mxr', 1, 0, 0), ('mxr', 1, 0, 1), ('mxr', 1, 2, 3), ('lm', 1, 3, 4, 0, 128, 'v'), ('lm', 1, 2, 3, 0, 128, 'v'), ('fin', 1, 0, 2, 0, 128), ('fin', 1, 2, 3, 0, 128), ('fin', 1, 3, 4, 0, 128)]
         pool = [('lm', 0, 0, 4, 0, 128, 'g'), ('lm', 1, 0, 2, 0, 128, 'g')]
         sp = [('st', 0, 0, 4), ('st', 1, 0, 2), ('st', 1, 2, 4)]
 
         fns = dict(wp=wp, wsp=wsp, tr=tr, xc=xc, xq=xq, mx1=mx1, relu=relu, hi=hi, hq=hq, si=si, sq=sq, ui=ui, uq=uq, mxu=mxu, ucp=ucp, utr=utr, mx2=mx2, mxr=mxr, lm=lm, fin=fin, st=st, bperm=bperm, btr=btr, bcopy=bcopy, ltr=ltr, lcopy=lcopy, dm=dm)
 
         def strip(n):
-            return n[:-1] if n[0] in ("xc", "si", "ui", "lm", "hi") else n
+            return n[:-1] if n[0] in ("xc", "si", "ui", "lm", "hi", "bcopy") else n
 
         tr_ring, acc_ring = [], []
         for n in pe:
@@ -392,7 +395,7 @@ def tile_marginal_relevance_slates_s9_kernel(tc, x, w_words, w_scales, b, users,
             elif k == "hq":
                 r += [("hi", n[1], n[2])]
             elif k == "sq":
-                r += [m[:-1] for m in act + dve + pool if m[0] == "si" and m[1] == n[1] and n[2] <= m[2] < n[2] + n[3]]
+                r += [m[:-1] for m in act + dve + pool if m[0] == "si" and m[1] == n[1] and m[2] == n[2] // 2]
             elif k == "uq":
                 r += [("ui",)]
             elif k == "mxu":

@@ -94,20 +94,20 @@ def tile_marginal_relevance_slates_s9_kernel(tc, x, w_words, w_scales, b, users,
 
         load_rows()
         load_x(0, 0, 1)
+        load_x(0, 0, 0)
+        load_x(0, 1, 1)
         load_ws()
         load_x(0, 1, 0)
-        load_x(0, 1, 1)
-        load_x(0, 0, 0)
+        load_w(1)
+        load_x(1, 0, 0)
+        load_selected(1, 0)
+        load_w(0)
+        load_x(1, 0, 1)
         load_x(1, 1, 1)
         load_x(1, 1, 0)
-        load_w(1)
-        load_selected(0, 1)
-        load_w(0)
-        load_x(1, 0, 0)
-        load_x(1, 0, 1)
-        load_selected(1, 0)
-        load_selected(1, 1)
         load_selected(0, 0)
+        load_selected(0, 1)
+        load_selected(1, 1)
         for h in range(H):
             for t in range(T):
                 nc.sync.dma_start(out=use_raw[:, h, t, :], in_=use_view[h, t])
@@ -338,10 +338,10 @@ def tile_marginal_relevance_slates_s9_kernel(tc, x, w_words, w_scales, b, users,
             for i in range(n):
                 nc.tensor.matmul(bank[:], lhsT=zero[:, 0:128], rhs=zero[:], start=True, stop=True)
 
-        TRB, ACB = 4, 4
-        pe = [('dm', 7, 0), ('tr', 0, 1, 1), ('tr', 0, 0, 1), ('tr', 0, 2, 0), ('tr', 0, 3, 0), ('dm', 2, 1), ('tr', 0, 2, 1), ('tr', 0, 3, 1), ('tr', 0, 0, 0), ('tr', 0, 1, 0), ('tr', 1, 2, 1), ('tr', 1, 2, 0), ('tr', 1, 3, 1), ('tr', 1, 3, 0), ('btr',), ('dm', 4, 2), ('mx1', 0, 1, 1, 0), ('mx1', 0, 1, 1, 1), ('mx1', 0, 1, 1, 2), ('mx1', 0, 1, 1, 3), ('mx1', 0, 1, 3, 0), ('mx1', 0, 1, 3, 1), ('mx1', 0, 1, 0, 0), ('mx1', 0, 1, 0, 1), ('mx1', 0, 1, 0, 2), ('mx1', 0, 1, 0, 3), ('mx1', 0, 1, 3, 2), ('mx1', 0, 1, 3, 3), ('mx1', 0, 1, 2, 0), ('mx1', 0, 1, 2, 1), ('mx1', 0, 1, 2, 2), ('mx1', 0, 1, 2, 3), ('mx1', 0, 0, 1, 0), ('mx1', 0, 0, 1, 1), ('tr', 1, 0, 0), ('tr', 1, 1, 0), ('tr', 1, 0, 1), ('tr', 1, 1, 1), ('mx1', 0, 0, 1, 2), ('mx1', 0, 0, 1, 3), ('mx1', 0, 0, 0, 0), ('mx1', 0, 0, 0, 1), ('mx1', 0, 0, 3, 0), ('mx1', 0, 0, 3, 1), ('mx1', 0, 0, 2, 0), ('mx1', 0, 0, 2, 1), ('mx1', 0, 0, 0, 2), ('mx1', 0, 0, 0, 3), ('mx1', 0, 0, 3, 2), ('mx1', 0, 0, 3, 3), ('mx1', 1, 1, 3, 0), ('mx1', 1, 1, 3, 1), ('mx1', 0, 0, 2, 2), ('mx1', 0, 0, 2, 3), ('mx1', 1, 1, 2, 0), ('mx1', 1, 1, 2, 1), ('mx1', 1, 1, 3, 2), ('mx1', 1, 1, 3, 3), ('mx1', 1, 1, 0, 0), ('mx1', 1, 1, 0, 1), ('mx1', 1, 1, 2, 2), ('mx1', 1, 1, 2, 3), ('mx1', 1, 1, 1, 0), ('mx1', 1, 1, 1, 1), ('mx1', 1, 1, 0, 2), ('mx1', 1, 1, 0, 3), ('mx1', 1, 1, 1, 2), ('mx1', 1, 1, 1, 3), ('mx1', 1, 0, 0, 0), ('mx1', 1, 0, 0, 1), ('mx2', 0, 2, 2), ('mx1', 1, 0, 0, 2), ('mx1', 1, 0, 0, 3), ('mx2', 0, 1, 2), ('mx2', 0, 0, 3), ('mx2', 0, 3, 3), ('mx2', 0, 2, 3), ('ltr',), ('mx2', 0, 0, 2), ('mx2', 0, 1, 3), ('mx1', 1, 0, 1, 0), ('mx1', 1, 0, 1, 1), ('mx2', 0, 3, 2), ('mx1', 1, 0, 1, 2), ('mx1', 1, 0, 1, 3), ('mx1', 1, 0, 2, 0), ('mx1', 1, 0, 2, 1), ('mx1', 1, 0, 2, 2), ('mx1', 1, 0, 2, 3), ('mx2', 0, 3, 1), ('mx2', 0, 1, 1), ('mx2', 0, 2, 0), ('mx1', 1, 0, 3, 0), ('mx1', 1, 0, 3, 1), ('mx1', 1, 0, 3, 2), ('mx1', 1, 0, 3, 3), ('mx2', 0, 1, 0), ('mx2', 0, 2, 1), ('mx2', 0, 0, 0), ('mxu', 0), ('mx2', 0, 3, 0), ('mx2', 0, 0, 1), ('mx2', 1, 2, 0), ('mx2', 1, 3, 1), ('mxu', 1), ('mx2', 1, 1, 1), ('mx2', 1, 0, 3), ('mx2', 1, 3, 0), ('mx2', 1, 0, 2), ('mx2', 1, 3, 2), ('mx2', 1, 1, 0), ('mx2', 1, 1, 3), ('mx2', 1, 1, 2), ('mx2', 1, 2, 1), ('utr', 0), ('mx2', 1, 2, 2), ('mx2', 1, 3, 3), ('mx2', 1, 0, 0), ('mx2', 1, 0, 1), ('mx2', 1, 2, 3), ('utr', 1)]
-        act = [('bperm',), ('xc', 0, 0, 0, 's'), ('xc', 0, 1, 0, 's'), ('xc', 1, 2, 1, 's'), ('xc', 1, 2, 0, 's'), ('xc', 1, 3, 0, 's'), ('relu', 0, 1, 1), ('si', 0, 1, 1, 1, 's'), ('relu', 0, 1, 0), ('relu', 0, 1, 3), ('relu', 0, 1, 2), ('xc', 1, 0, 0, 's'), ('xc', 1, 0, 1, 's'), ('xc', 1, 1, 1, 's'), ('relu', 0, 0, 1), ('si', 1, 0, 0, 1, 's'), ('relu', 0, 0, 0), ('relu', 0, 0, 3), ('relu', 0, 0, 2), ('hi', 0, 0, 's'), ('relu', 1, 1, 3), ('relu', 1, 1, 2), ('relu', 1, 1, 0), ('relu', 1, 1, 1), ('relu', 1, 0, 0), ('si', 0, 0, 0, 3, 's'), ('hi', 1, 1, 's'), ('relu', 1, 0, 1), ('relu', 1, 0, 2), ('ui', 's'), ('relu', 1, 0, 3), ('lcopy',), ('hi', 1, 0, 's'), ('ucp', 0), ('ucp', 1)]
-        dve = [('wsp',), ('xc', 0, 1, 1, 'v'), ('xc', 0, 0, 1, 'v'), ('xc', 0, 2, 0, 'v'), ('xc', 0, 3, 0, 'v'), ('xc', 0, 2, 1, 'v'), ('xc', 0, 3, 1, 'v'), ('xq', 0, 2, 2), ('xq', 0, 0, 2), ('wp', 1), ('xc', 1, 3, 1, 'v'), ('bcopy', 'v'), ('xq', 1, 2, 2), ('si', 0, 1, 2, 2, 'v'), ('wp', 0), ('si', 0, 1, 0, 1, 'v'), ('sq', 0, 2, 2), ('hi', 0, 1, 'v'), ('xc', 1, 1, 0, 'v'), ('hq', 0, 1), ('xq', 1, 0, 2), ('si', 1, 0, 1, 3, 'v'), ('si', 1, 1, 0, 4, 'v'), ('hq', 0, 0), ('sq', 1, 2, 2), ('si', 0, 0, 3, 1, 'v'), ('sq', 1, 0, 2), ('mxr', 0, 2, 2), ('mxr', 0, 1, 2), ('mxr', 0, 0, 3), ('mxr', 0, 3, 3), ('mxr', 0, 2, 3), ('mxr', 0, 0, 2), ('mxr', 0, 1, 3), ('sq', 0, 0, 2), ('mxr', 0, 3, 2), ('hq', 1, 1), ('mxr', 0, 3, 1), ('mxr', 0, 1, 1), ('uq',), ('mxr', 0, 2, 0), ('mxr', 0, 1, 0), ('mxr', 0, 2, 1), ('mxr', 0, 0, 0), ('hq', 1, 0), ('mxr', 0, 3, 0), ('mxr', 0, 0, 1), ('mxr', 1, 2, 0), ('mxr', 1, 3, 1), ('mxr', 1, 1, 1), ('mxr', 1, 0, 3), ('mxr', 1, 3, 0), ('mxr', 1, 0, 2), ('mxr', 1, 3, 2), ('mxr', 1, 1, 0), ('mxr', 1, 1, 2), ('mxr', 1, 2, 1), ('mxr', 1, 1, 3), ('fin', 0, 0, 4, 0, 128), ('mxr', 1, 2, 2), ('mxr', 1, 3, 3), ('mxr', 1, 0, 0), ('mxr', 1, 0, 1), ('mxr', 1, 2, 3), ('lm', 1, 3, 4, 0, 128, 'v'), ('lm', 1, 2, 3, 0, 128, 'v'), ('fin', 1, 0, 2, 0, 128), ('fin', 1, 2, 3, 0, 128), ('fin', 1, 3, 4, 0, 128)]
+        TRB, ACB = 3, 5
+        pe = [('dm', 7, 0), ('tr', 0, 1, 1), ('tr', 0, 0, 1), ('tr', 0, 1, 0), ('tr', 0, 0, 0), ('dm', 2, 1), ('tr', 0, 2, 1), ('tr', 0, 3, 1), ('tr', 0, 2, 0), ('tr', 0, 3, 0), ('btr',), ('dm', 4, 2), ('mx1', 0, 1, 0, 0), ('mx1', 0, 1, 0, 1), ('tr', 1, 0, 0), ('tr', 1, 1, 0), ('mx1', 0, 1, 0, 2), ('mx1', 0, 1, 0, 3), ('mx1', 0, 1, 3, 0), ('mx1', 0, 1, 3, 1), ('mx1', 0, 1, 3, 2), ('mx1', 0, 1, 3, 3), ('mx1', 0, 1, 2, 0), ('mx1', 0, 1, 2, 1), ('mx1', 0, 1, 2, 2), ('mx1', 0, 1, 2, 3), ('mx1', 0, 1, 1, 0), ('mx1', 0, 1, 1, 1), ('mx1', 0, 1, 1, 2), ('mx1', 0, 1, 1, 3), ('tr', 1, 0, 1), ('tr', 1, 1, 1), ('tr', 1, 2, 1), ('mx1', 0, 0, 3, 0), ('mx1', 0, 0, 3, 1), ('mx1', 0, 0, 3, 2), ('mx1', 0, 0, 3, 3), ('tr', 1, 3, 0), ('tr', 1, 3, 1), ('tr', 1, 2, 0), ('mx1', 0, 0, 2, 0), ('mx1', 0, 0, 2, 1), ('mx1', 0, 0, 2, 2), ('mx1', 0, 0, 2, 3), ('mx1', 0, 0, 1, 0), ('mx1', 0, 0, 1, 1), ('mx1', 0, 0, 1, 2), ('mx1', 0, 0, 1, 3), ('mx1', 1, 0, 3, 0), ('mx1', 1, 0, 3, 1), ('mx1', 0, 0, 0, 0), ('mx1', 0, 0, 0, 1), ('mx1', 0, 0, 0, 2), ('mx1', 0, 0, 0, 3), ('ltr',), ('mx1', 1, 0, 3, 2), ('mx1', 1, 0, 3, 3), ('mx1', 1, 1, 2, 0), ('mx1', 1, 1, 2, 1), ('mx1', 1, 0, 2, 0), ('mx1', 1, 0, 2, 1), ('mx1', 1, 0, 2, 2), ('mx1', 1, 0, 2, 3), ('mx1', 1, 1, 2, 2), ('mx1', 1, 1, 2, 3), ('mx1', 1, 0, 0, 0), ('mx1', 1, 0, 0, 1), ('mx1', 1, 0, 0, 2), ('mx1', 1, 0, 0, 3), ('mx2', 0, 0, 1), ('mx2', 0, 3, 0), ('mx2', 0, 0, 0), ('mx1', 1, 0, 1, 0), ('mx1', 1, 0, 1, 1), ('mx1', 1, 0, 1, 2), ('mx1', 1, 0, 1, 3), ('mx2', 0, 2, 1), ('mx2', 0, 2, 0), ('mx2', 0, 1, 1), ('mx1', 1, 1, 1, 0), ('mx1', 1, 1, 1, 1), ('mx1', 1, 1, 1, 2), ('mx1', 1, 1, 1, 3), ('mx2', 0, 1, 0), ('mx1', 1, 1, 0, 0), ('mx1', 1, 1, 0, 1), ('mx1', 1, 1, 3, 0), ('mx1', 1, 1, 3, 1), ('mx1', 1, 1, 0, 2), ('mx1', 1, 1, 0, 3), ('mx1', 1, 1, 3, 2), ('mx1', 1, 1, 3, 3), ('mx2', 0, 0, 2), ('mx2', 0, 3, 3), ('mx2', 0, 1, 2), ('mx2', 0, 1, 3), ('mxu', 0), ('mx2', 0, 3, 1), ('mx2', 0, 0, 3), ('mx2', 0, 2, 3), ('mx2', 0, 3, 2), ('mx2', 1, 3, 3), ('mx2', 1, 1, 1), ('mx2', 1, 0, 2), ('mx2', 1, 1, 2), ('mx2', 0, 2, 2), ('mx2', 1, 0, 3), ('mx2', 1, 0, 0), ('mx2', 1, 1, 3), ('mx2', 1, 1, 0), ('mx2', 1, 3, 2), ('mx2', 1, 0, 1), ('utr', 0), ('mxu', 1), ('mx2', 1, 3, 1), ('mx2', 1, 2, 0), ('mx2', 1, 2, 2), ('mx2', 1, 3, 0), ('mx2', 1, 2, 3), ('mx2', 1, 2, 1), ('utr', 1)]
+        act = [('bperm',), ('xc', 0, 0, 0, 's'), ('xc', 0, 2, 1, 's'), ('xc', 0, 3, 1, 's'), ('xc', 0, 2, 0, 's'), ('xc', 0, 3, 0, 's'), ('xc', 1, 1, 0, 's'), ('relu', 0, 1, 0), ('relu', 0, 1, 3), ('relu', 0, 1, 2), ('relu', 0, 1, 1), ('xc', 1, 0, 1, 's'), ('xc', 1, 1, 1, 's'), ('xc', 1, 2, 1, 's'), ('relu', 0, 0, 3), ('xc', 1, 3, 0, 's'), ('xc', 1, 2, 0, 's'), ('si', 0, 0, 3, 1, 's'), ('relu', 0, 0, 2), ('relu', 0, 0, 1), ('relu', 0, 0, 0), ('relu', 1, 0, 3), ('si', 1, 1, 2, 1, 's'), ('relu', 1, 1, 2), ('relu', 1, 0, 2), ('relu', 1, 0, 0), ('si', 1, 1, 3, 1, 's'), ('relu', 1, 0, 1), ('hi', 1, 0, 's'), ('si', 1, 1, 1, 1, 's'), ('ui', 's'), ('relu', 1, 1, 1), ('relu', 1, 1, 0), ('relu', 1, 1, 3), ('hi', 1, 1, 's'), ('lcopy',), ('ucp', 0), ('ucp', 1)]
+        dve = [('xc', 0, 1, 1, 'v'), ('xc', 0, 0, 1, 'v'), ('xc', 0, 1, 0, 'v'), ('wsp',), ('xq', 0, 0, 2), ('wp', 1), ('bcopy', 'v'), ('xq', 0, 2, 2), ('xc', 1, 0, 0, 'v'), ('si', 1, 0, 0, 1, 'v'), ('si', 1, 0, 1, 3, 'v'), ('wp', 0), ('sq', 1, 0, 2), ('hi', 0, 1, 'v'), ('xq', 1, 0, 2), ('hq', 0, 1), ('xc', 1, 3, 1, 'v'), ('si', 0, 0, 0, 3, 'v'), ('xq', 1, 2, 2), ('si', 0, 1, 0, 1, 'v'), ('si', 0, 1, 2, 1, 'v'), ('hi', 0, 0, 'v'), ('sq', 0, 0, 2), ('hq', 0, 0), ('si', 1, 1, 0, 1, 'v'), ('si', 0, 1, 1, 1, 'v'), ('si', 0, 1, 3, 1, 'v'), ('mxr', 0, 0, 0), ('mxr', 0, 0, 1), ('mxr', 0, 3, 0), ('sq', 0, 2, 2), ('mxr', 0, 1, 1), ('mxr', 0, 2, 1), ('mxr', 0, 2, 0), ('sq', 1, 2, 2), ('hq', 1, 0), ('mxr', 0, 1, 0), ('uq',), ('mxr', 0, 3, 3), ('mxr', 0, 0, 2), ('mxr', 0, 1, 3), ('mxr', 0, 1, 2), ('hq', 1, 1), ('mxr', 0, 0, 3), ('mxr', 0, 3, 1), ('mxr', 1, 3, 3), ('mxr', 0, 2, 3), ('mxr', 0, 3, 2), ('mxr', 1, 0, 2), ('mxr', 1, 1, 1), ('mxr', 0, 2, 2), ('mxr', 1, 1, 2), ('mxr', 1, 0, 0), ('mxr', 1, 0, 3), ('mxr', 1, 1, 0), ('mxr', 1, 1, 3), ('fin', 0, 0, 4, 0, 128), ('mxr', 1, 3, 2), ('mxr', 1, 0, 1), ('mxr', 1, 2, 0), ('mxr', 1, 3, 1), ('mxr', 1, 3, 0), ('mxr', 1, 2, 2), ('fin', 1, 0, 2, 0, 128), ('mxr', 1, 2, 3), ('mxr', 1, 2, 1), ('lm', 1, 3, 4, 0, 128, 'v'), ('lm', 1, 2, 3, 0, 128, 'v'), ('fin', 1, 3, 4, 0, 128), ('fin', 1, 2, 3, 0, 128)]
         pool = [('lm', 0, 0, 4, 0, 128, 'g'), ('lm', 1, 0, 2, 0, 128, 'g')]
         sp = [('st', 0, 0, 4), ('st', 1, 0, 2), ('st', 1, 2, 4)]
 

from contextlib import ExitStack

import concourse.mybir as mybir
from concourse.masks import make_identity

F32 = mybir.dt.float32
BF16 = mybir.dt.bfloat16
I32 = mybir.dt.int32
U32 = mybir.dt.uint32
U8 = mybir.dt.uint8
E4M3 = mybir.dt.float8_e4m3fn_x4
E5M2 = mybir.dt.float8_e5m2_x4
E2M1 = mybir.dt.float4_e2m1fn_x4
ALU = mybir.AluOpType
ACT = mybir.ActivationFunctionType
AXES = mybir.AxisListType

TOKENS, K, F, USERS, SLATE = 1024, 2048, 1024, 128, 16
FLOPS = 2 * TOKENS * K * F + 2 * TOKENS * F * (USERS + USERS * SLATE)

P = 128
SLABS = 2
R = 4
G = 4
H = 2
T = 4
N = 512


def tile_marginal_relevance_slates_s9_kernel(tc, x, w_words, w_scales, b, users, selected, lam, out):
    nc = tc.nc
    with ExitStack() as ctx:
        keep = ctx.enter_context(tc.tile_pool(name="keep", bufs=1))
        work = ctx.enter_context(tc.tile_pool(name="work", bufs=2))
        psum = ctx.enter_context(tc.psum_pool(name="psum", bufs=1))
        ctx.enter_context(tc.manual_schedule())

        x_view = x.rearrange("(s p r) k -> s p r k", s=SLABS, r=R)
        x_raw = {}

        def load_x(s, gp, rp):
            t = keep.tile([P, 2, 1024], BF16, name="xraw_%d_%d_%d" % (s, gp, rp))
            nc.sync.dma_start(out=t[:], in_=x_view[s][:, 2 * rp : 2 * rp + 2, 1024 * gp : 1024 * gp + 1024])
            x_raw[s, gp, rp] = t

        w_raw = keep.tile([P, H, G * 1024], U8, name="w_raw", align_bytes=64)
        w_perm = keep.tile([P, H, G * 1024], U8, name="w_perm", align_bytes=64)
        ws_raw = keep.tile([P, G * 1024], U8, name="ws_raw", align_bytes=64)
        ws_perm = keep.tile([P, G * 1024], U8, name="ws_perm", align_bytes=64)
        w_view = w_words.bitcast(I32).rearrange("g p (h n) -> h p g n", h=H)
        ws_view = w_scales.bitcast(I32).rearrange("g r n -> r g n")
        ws_raw_i = ws_raw[:].bitcast(I32).rearrange("p (g n) -> p g n", g=G)

        def load_w(h):
            nc.sync.dma_start(out=w_raw[:, h, :].bitcast(I32).rearrange("p (g n) -> p g n", g=G), in_=w_view[h])

        def load_ws():
            for q in range(4):
                nc.sync.dma_start(out=ws_raw_i[32 * q : 32 * q + 4], in_=ws_view[4 * q : 4 * q + 4])

        b_rows = keep.tile([P, N], BF16, name="b_rows")
        b_perm = keep.tile([P, T, P], BF16, name="b_perm")
        lam_rows = keep.tile([P, P], BF16, name="lam_rows")
        ones = keep.tile([P, P], BF16, name="ones")
        sel_view = selected.rearrange("(h j t i) c -> h t j i c", h=H, t=T, i=4)
        use_view = users.rearrange("(h j t i) c -> h t j i c", h=H, t=T, i=4)
        sel_raw = [[keep.tile([P, T, 1024], BF16, name="sel_raw%d%d" % (h, half)) for half in range(2)] for h in range(H)]
        use_raw = keep.tile([P, H, T, USERS], BF16, name="use_raw")

        def load_selected(h, half):
            c = slice(1024 * half, 1024 * half + 1024)
            for t in range(T):
                nc.sync.dma_start(out=sel_raw[h][half][:, t, :], in_=sel_view[h, t][:, :, c])

        def load_rows():
            nc.sync.dma_start(out=b_rows[0:H, :], in_=b.rearrange("(h n) -> h n", h=H))
            nc.sync.dma_start(out=lam_rows[0:1, :], in_=lam.rearrange("(o u) -> o u", o=1))

        nc.vector.memset(b_rows[:], 0.0)
        nc.vector.memset(lam_rows[:], 0.0)
        nc.vector.memset(ws_raw[:].bitcast(I32), 0)
        nc.vector.memset(ones[:], 1.0)
        ident_b = keep.tile([P, P], BF16, name="ident_b")
        bias = keep.tile([P, H, T], F32, name="bias")
        lam_row = keep.tile([P, USERS], F32, name="lam_row")
        zero = keep.tile([P, N], BF16, name="zero")
        nc.gpsimd.memset(zero[:], 0.0)
        ident = keep.tile([P, P], F32, name="ident")
        make_identity(nc, ident[:])
        warm = keep.tile([P, 1], F32, name="warm")
        nc.vector.memset(warm[:], 0.0)
        nc.scalar.activation(out=warm[:], in_=warm[:], func=ACT.Relu)
        nc.vector.tensor_copy(out=ident_b[:], in_=ident[:])

        load_rows()
        load_x(0, 0, 1)
        load_x(0, 0, 0)
        load_x(0, 1, 1)
        load_ws()
        load_x(0, 1, 0)
        load_w(1)
        load_x(1, 0, 0)
        load_selected(1, 0)
        load_w(0)
        load_x(1, 0, 1)
        load_x(1, 1, 1)
        load_x(1, 1, 0)
        load_selected(0, 0)
        load_selected(0, 1)
        load_selected(1, 1)
        for h in range(H):
            for t in range(T):
                nc.sync.dma_start(out=use_raw[:, h, t, :], in_=use_view[h, t])


        def wp(h):
            src = w_raw[:, h, :].bitcast(I32).rearrange("p (g j t w) -> p g t j w", j=32, t=T, w=2)
            dst = w_perm[:, h, :].bitcast(I32).rearrange("p (g t j w) -> p g t j w", j=32, t=T, w=2)
            nc.vector.tensor_copy(out=dst, in_=src)

        def wsp():
            src = ws_raw[:].bitcast(I32).rearrange("p (q j t) -> p q t j", j=32, t=T)
            dst = ws_perm[:].bitcast(I32).rearrange("p (q t j) -> p q t j", j=32, t=T)
            nc.vector.tensor_copy(out=dst, in_=src)

        x_codes = [keep.tile([P, G * N], U32, name="x_codes%d" % s, align_bytes=64) for s in range(SLABS)]
        x_scales = [keep.tile([P, G * N], U8, name="x_scales%d" % s, align_bytes=64) for s in range(SLABS)]
        x_in = {}
        x_bank = {}

        def tr(s, g, rp):
            words = x_raw[s, g // 2, rp][:].rearrange("p r k -> p (r k)").bitcast(F32)
            bank = psum.tile([P, N], F32, name="tr", bufs=TRB)
            x_bank[s, g, rp] = bank
            for r in range(2):
                for u in range(2):
                    w0 = 512 * r + 256 * (g % 2) + u
                    c0 = 256 * r + 128 * u
                    nc.tensor.transpose(bank[:, c0 : c0 + 128], words[:, w0 : w0 + 255 : 2], ident[:])

        def xc(s, g, rp, e):
            if (s, g // 2) not in x_in:
                x_in[s, g // 2] = work.tile([P, 2, N * T], BF16, name="x_in", align_bytes=64, bufs=4)
            dst = x_in[s, g // 2][:, g % 2].bitcast(F32).rearrange("p (r n u) -> p r n u", r=R, u=2)[:, 2 * rp : 2 * rp + 2]
            src = x_bank[s, g, rp][:].rearrange("p (r u n) -> p r n u", r=2, u=2)
            if e == "v":
                nc.vector.tensor_copy(out=dst, in_=src)
            else:
                nc.scalar.copy(out=dst, in_=src)

        def xq(s, g, ng):
            c = slice(g * N, (g + ng) * N)
            src = x_in[s, g // 2][:, g % 2 : g % 2 + ng].rearrange("p g k -> p (g k)")
            nc.vector.quantize_mx(out=x_codes[s][:, c].bitcast(E4M3), scales=x_scales[s][:, c], in_=src)

        acc1 = {}
        h_raw = {}
        h_in = {}

        def mx1(s, h, t, g):
            if g == 0:
                acc1[s, h, t] = psum.tile([P, N], F32, name="acc", bufs=ACB)
            q = g * T + t
            qs = (g * H + h) * T + t
            c = slice(g * N, (g + 1) * N)
            nc.tensor.matmul_mx(
                out=acc1[s, h, t][:],
                lhsT=w_perm[:, h, 256 * q : 256 * q + 256].bitcast(E2M1),
                lhsT_scale=ws_perm[:, 128 * qs : 128 * qs + 128],
                rhs=x_codes[s][:, c].bitcast(E4M3),
                rhs_scale=x_scales[s][:, c],
                start=(g == 0),
                stop=(g == G - 1),
            )

        def relu(s, h, t):
            if (s, h) not in h_raw:
                h_raw[s, h] = work.tile([P, 2, N, 2], BF16, name="h_raw", bufs=2)
            nc.scalar.activation(
                out=h_raw[s, h][:, t // 2, :, t % 2], in_=acc1[s, h, t][:], func=ACT.Relu, bias=bias[:, h, t : t + 1], scale=1.0
            )

        h_codes = [keep.tile([P, H * N], U32, name="h_codes%d" % s, align_bytes=64) for s in range(SLABS)]
        h_scales = [keep.tile([P, H * N], U8, name="h_scales%d" % s, align_bytes=64) for s in range(SLABS)]

        def hi(s, h, e):
            h_in[s, h] = work.tile([P, N, T], BF16, name="h_in", align_bytes=64, bufs=2)
            words = h_raw[s, h][:].rearrange("p a n e -> p (a n e)").bitcast(F32).rearrange("p (a n) -> p n a", a=2)
            dst = h_in[s, h][:].rearrange("p n t -> p (n t)").bitcast(F32).rearrange("p (n a) -> p n a", a=2)
            if e == "v":
                nc.vector.tensor_copy(out=dst, in_=words)
            else:
                nc.scalar.copy(out=dst, in_=words)

        def hq(s, h):
            c = slice(h * N, (h + 1) * N)
            nc.vector.quantize_mx(
                out=h_codes[s][:, c].bitcast(E5M2), scales=h_scales[s][:, c], in_=h_in[s, h][:].rearrange("p n t -> p (n t)")
            )

        sel_codes = [keep.tile([P, SLATE * USERS], U32, name="sel_codes%d" % h, align_bytes=64) for h in range(H)]
        sel_scales = [keep.tile([P, SLATE * USERS], U8, name="sel_scales%d" % h, align_bytes=64) for h in range(H)]
        use_codes = keep.tile([P, H * USERS], U32, name="use_codes", align_bytes=64)
        use_scales = keep.tile([P, H * USERS], U8, name="use_scales", align_bytes=64)
        s_in = {}

        def si(h, half, q0, nq, e):
            if (h, half) not in s_in:
                s_in[h, half] = work.tile([P, 1024, T], BF16, name="s_in", align_bytes=64, bufs=4)
            c = slice(256 * q0, 256 * (q0 + nq))
            dst = s_in[h, half][:, c].rearrange("p (c i) t -> p c t i", i=4)
            src = sel_raw[h][half][:, :, c].rearrange("p t (c i) -> p c t i", i=4)
            if e == "v":
                nc.vector.tensor_copy(out=dst, in_=src)
            else:
                nc.scalar.copy(out=dst, in_=src)

        def sq(h, k, nk):
            c = slice(N * k, N * k + N * nk)
            src = s_in[h, k // 2][:, N * (k % 2) : N * (k % 2 + nk)].rearrange("p c t -> p (c t)")
            nc.vector.quantize_mx(out=sel_codes[h][:, c].bitcast(E4M3), scales=sel_scales[h][:, c], in_=src)

        u_in = {}

        def ui(e):
            u_in[0] = work.tile([P, H, USERS, T], BF16, name="u_in", align_bytes=64, bufs=1)
            src = use_raw[:].rearrange("p h t u -> p h u t")
            if e == "v":
                nc.vector.tensor_copy(out=u_in[0][:], in_=src)
            else:
                nc.scalar.copy(out=u_in[0][:], in_=src)

        def uq():
            nc.vector.quantize_mx(
                out=use_codes[:].bitcast(E4M3), scales=use_scales[:], in_=u_in[0][:].rearrange("p h u t -> p (h u t)")
            )

        acc2 = {}
        rel_t = {}
        rel = {}
        red = [keep.tile([P, R, USERS], F32, name="red%d" % s) for s in range(SLABS)]

        def mxu(s):
            acc2[s, "u"] = psum.tile([P, N], F32, name="acc", bufs=ACB)
            for h in range(H):
                m = slice(h * N, (h + 1) * N)
                nc.tensor.matmul_mx(
                    out=acc2[s, "u"][:],
                    lhsT=use_codes[:, USERS * h : USERS * h + USERS].bitcast(E4M3),
                    lhsT_scale=use_scales[:, USERS * h : USERS * h + USERS],
                    rhs=h_codes[s][:, m].bitcast(E5M2),
                    rhs_scale=h_scales[s][:, m],
                    start=(h == 0),
                    stop=(h == H - 1),
                )

        def ucp(s):
            rel_t[s] = work.tile([P, N], F32, name="rel_t", bufs=2)
            nc.scalar.copy(out=rel_t[s][:], in_=acc2[s, "u"][:])

        def utr(s):
            rel[s] = psum.tile([P, N], F32, name="tr", bufs=TRB)
            for r in range(R):
                c = slice(128 * r, 128 * r + 128)
                nc.tensor.transpose(rel[s][:, c], rel_t[s][:, c], ident[:])

        def mx2(s, r, k):
            acc2[s, r, k] = psum.tile([P, N], F32, name="acc", bufs=ACB)
            for h in range(H):
                m = slice(h * N + 128 * r, h * N + 128 * r + 128)
                c = slice(512 * k, 512 * k + 512)
                nc.tensor.matmul_mx(
                    out=acc2[s, r, k][:],
                    lhsT=h_codes[s][:, m].bitcast(E5M2),
                    lhsT_scale=h_scales[s][:, m],
                    rhs=sel_codes[h][:, c].bitcast(E4M3),
                    rhs_scale=sel_scales[h][:, c],
                    start=(h == 0),
                    stop=(h == H - 1),
                )

        def mxr(s, r, k):
            nc.vector.tensor_reduce(
                out=red[s][:, r, 32 * k : 32 * k + 32],
                in_=acc2[s, r, k][:].rearrange("p (u j) -> p u j", j=SLATE),
                op=ALU.max,
                axis=AXES.X,
            )

        out_view = out.rearrange("(s p r) u -> s p r u", s=SLABS, r=R)

        def lam_view(r0, r1, u0, u1):
            return lam_row[:, u0:u1].unsqueeze(1).to_broadcast([P, r1 - r0, u1 - u0])

        def lm(s, r0, r1, u0, u1, e):
            d = red[s][:, r0:r1, u0:u1]
            eng = nc.vector if e == "v" else nc.gpsimd
            eng.tensor_tensor(out=d, in0=d, in1=lam_view(r0, r1, u0, u1), op=ALU.mult)

        def fin(s, r0, r1, u0, u1):
            nc.vector.tensor_tensor(
                out=red[s][:, r0:r1, u0:u1],
                in0=rel[s][:].rearrange("p (r u) -> p r u", r=R)[:, r0:r1, u0:u1],
                in1=red[s][:, r0:r1, u0:u1],
                op=ALU.subtract,
            )

        def st(s, r0, r1):
            nc.sync.dma_start(out=out_view[s][:, r0:r1], in_=red[s][:, r0:r1])

        def bperm():
            nc.scalar.copy(
                out=b_perm[:].rearrange("p t (j i) -> p t j i", i=4),
                in_=b_rows[:].rearrange("p (j t i) -> p t j i", t=T, i=4),
            )

        def btr():
            x_bank["b"] = psum.tile([P, T, P], BF16, name="tr", bufs=TRB)
            for t in range(T):
                nc.tensor.transpose(x_bank["b"][:, t, :], b_perm[:, t, :], ident_b[:])

        def bcopy(e):
            src = x_bank["b"][:, :, 0:H].rearrange("p t h -> p h t")
            if e == "v":
                nc.vector.tensor_copy(out=bias[:], in_=src)
            else:
                nc.scalar.copy(out=bias[:], in_=src)

        def ltr():
            x_bank["l"] = psum.tile([P, P], F32, name="tr", bufs=TRB)
            nc.tensor.matmul(x_bank["l"][:], lhsT=ones[:], rhs=lam_rows[:], start=True, stop=True)

        def lcopy():
            nc.scalar.copy(out=lam_row[:], in_=x_bank["l"][:])

        def dm(n, key):
            bank = psum.tile([P, N], F32, name="tr", bufs=TRB)
            for i in range(n):
                nc.tensor.matmul(bank[:], lhsT=zero[:, 0:128], rhs=zero[:], start=True, stop=True)

        TRB, ACB = 3, 5
        pe = [('dm', 7, 0), ('tr', 0, 1, 1), ('tr', 0, 0, 1), ('tr', 0, 1, 0), ('tr', 0, 0, 0), ('dm', 2, 1), ('tr', 0, 2, 1), ('tr', 0, 3, 1), ('tr', 0, 2, 0), ('tr', 0, 3, 0), ('btr',), ('dm', 4, 2), ('mx1', 0, 1, 0, 0), ('mx1', 0, 1, 0, 1), ('tr', 1, 0, 0), ('tr', 1, 1, 0), ('mx1', 0, 1, 0, 2), ('mx1', 0, 1, 0, 3), ('mx1', 0, 1, 3, 0), ('mx1', 0, 1, 3, 1), ('mx1', 0, 1, 3, 2), ('mx1', 0, 1, 3, 3), ('mx1', 0, 1, 2, 0), ('mx1', 0, 1, 2, 1), ('mx1', 0, 1, 2, 2), ('mx1', 0, 1, 2, 3), ('mx1', 0, 1, 1, 0), ('mx1', 0, 1, 1, 1), ('mx1', 0, 1, 1, 2), ('mx1', 0, 1, 1, 3), ('tr', 1, 0, 1), ('tr', 1, 1, 1), ('tr', 1, 2, 1), ('mx1', 0, 0, 3, 0), ('mx1', 0, 0, 3, 1), ('mx1', 0, 0, 3, 2), ('mx1', 0, 0, 3, 3), ('tr', 1, 3, 0), ('tr', 1, 3, 1), ('tr', 1, 2, 0), ('mx1', 0, 0, 2, 0), ('mx1', 0, 0, 2, 1), ('mx1', 0, 0, 2, 2), ('mx1', 0, 0, 2, 3), ('mx1', 0, 0, 1, 0), ('mx1', 0, 0, 1, 1), ('mx1', 0, 0, 1, 2), ('mx1', 0, 0, 1, 3), ('mx1', 1, 0, 3, 0), ('mx1', 1, 0, 3, 1), ('mx1', 0, 0, 0, 0), ('mx1', 0, 0, 0, 1), ('mx1', 0, 0, 0, 2), ('mx1', 0, 0, 0, 3), ('ltr',), ('mx1', 1, 0, 3, 2), ('mx1', 1, 0, 3, 3), ('mx1', 1, 1, 2, 0), ('mx1', 1, 1, 2, 1), ('mx1', 1, 0, 2, 0), ('mx1', 1, 0, 2, 1), ('mx1', 1, 0, 2, 2), ('mx1', 1, 0, 2, 3), ('mx1', 1, 1, 2, 2), ('mx1', 1, 1, 2, 3), ('mx1', 1, 0, 0, 0), ('mx1', 1, 0, 0, 1), ('mx1', 1, 0, 0, 2), ('mx1', 1, 0, 0, 3), ('mx2', 0, 0, 1), ('mx2', 0, 3, 0), ('mx2', 0, 0, 0), ('mx1', 1, 0, 1, 0), ('mx1', 1, 0, 1, 1), ('mx1', 1, 0, 1, 2), ('mx1', 1, 0, 1, 3), ('mx2', 0, 2, 1), ('mx2', 0, 2, 0), ('mx2', 0, 1, 1), ('mx1', 1, 1, 1, 0), ('mx1', 1, 1, 1, 1), ('mx1', 1, 1, 1, 2), ('mx1', 1, 1, 1, 3), ('mx2', 0, 1, 0), ('mx1', 1, 1, 0, 0), ('mx1', 1, 1, 0, 1), ('mx1', 1, 1, 3, 0), ('mx1', 1, 1, 3, 1), ('mx1', 1, 1, 0, 2), ('mx1', 1, 1, 0, 3), ('mx1', 1, 1, 3, 2), ('mx1', 1, 1, 3, 3), ('mx2', 0, 0, 2), ('mx2', 0, 3, 3), ('mx2', 0, 1, 2), ('mx2', 0, 1, 3), ('mxu', 0), ('mx2', 0, 3, 1), ('mx2', 0, 0, 3), ('mx2', 0, 2, 3), ('mx2', 0, 3, 2), ('mx2', 1, 3, 3), ('mx2', 1, 1, 1), ('mx2', 1, 0, 2), ('mx2', 1, 1, 2), ('mx2', 0, 2, 2), ('mx2', 1, 0, 3), ('mx2', 1, 0, 0), ('mx2', 1, 1, 3), ('mx2', 1, 1, 0), ('mx2', 1, 3, 2), ('mx2', 1, 0, 1), ('utr', 0), ('mxu', 1), ('mx2', 1, 3, 1), ('mx2', 1, 2, 0), ('mx2', 1, 2, 2), ('mx2', 1, 3, 0), ('mx2', 1, 2, 3), ('mx2', 1, 2, 1), ('utr', 1)]
        act = [('bperm',), ('xc', 0, 0, 0, 's'), ('xc', 0, 2, 1, 's'), ('xc', 0, 3, 1, 's'), ('xc', 0, 2, 0, 's'), ('xc', 0, 3, 0, 's'), ('xc', 1, 1, 0, 's'), ('relu', 0, 1, 0), ('relu', 0, 1, 3), ('relu', 0, 1, 2), ('relu', 0, 1, 1), ('xc', 1, 0, 1, 's'), ('xc', 1, 1, 1, 's'), ('xc', 1, 2, 1, 's'), ('relu', 0, 0, 3), ('xc', 1, 3, 0, 's'), ('xc', 1, 2, 0, 's'), ('si', 0, 0, 3, 1, 's'), ('relu', 0, 0, 2), ('relu', 0, 0, 1), ('relu', 0, 0, 0), ('relu', 1, 0, 3), ('si', 1, 1, 2, 1, 's'), ('relu', 1, 1, 2), ('relu', 1, 0, 2), ('relu', 1, 0, 0), ('si', 1, 1, 3, 1, 's'), ('relu', 1, 0, 1), ('hi', 1, 0, 's'), ('si', 1, 1, 1, 1, 's'), ('ui', 's'), ('relu', 1, 1, 1), ('relu', 1, 1, 0), ('relu', 1, 1, 3), ('hi', 1, 1, 's'), ('lcopy',), ('ucp', 0), ('ucp', 1)]
        dve = [('xc', 0, 1, 1, 'v'), ('xc', 0, 0, 1, 'v'), ('xc', 0, 1, 0, 'v'), ('wsp',), ('xq', 0, 0, 2), ('wp', 1), ('bcopy', 'v'), ('xq', 0, 2, 2), ('xc', 1, 0, 0, 'v'), ('si', 1, 0, 0, 1, 'v'), ('si', 1, 0, 1, 3, 'v'), ('wp', 0), ('sq', 1, 0, 2), ('hi', 0, 1, 'v'), ('xq', 1, 0, 2), ('hq', 0, 1), ('xc', 1, 3, 1, 'v'), ('si', 0, 0, 0, 3, 'v'), ('xq', 1, 2, 2), ('si', 0, 1, 0, 1, 'v'), ('si', 0, 1, 2, 1, 'v'), ('hi', 0, 0, 'v'), ('sq', 0, 0, 2), ('hq', 0, 0), ('si', 1, 1, 0, 1, 'v'), ('si', 0, 1, 1, 1, 'v'), ('si', 0, 1, 3, 1, 'v'), ('mxr', 0, 0, 0), ('mxr', 0, 0, 1), ('mxr', 0, 3, 0), ('sq', 0, 2, 2), ('mxr', 0, 1, 1), ('mxr', 0, 2, 1), ('mxr', 0, 2, 0), ('sq', 1, 2, 2), ('hq', 1, 0), ('mxr', 0, 1, 0), ('uq',), ('mxr', 0, 3, 3), ('mxr', 0, 0, 2), ('mxr', 0, 1, 3), ('mxr', 0, 1, 2), ('hq', 1, 1), ('mxr', 0, 0, 3), ('mxr', 0, 3, 1), ('mxr', 1, 3, 3), ('mxr', 0, 2, 3), ('mxr', 0, 3, 2), ('mxr', 1, 0, 2), ('mxr', 1, 1, 1), ('mxr', 0, 2, 2), ('mxr', 1, 1, 2), ('mxr', 1, 0, 0), ('mxr', 1, 0, 3), ('mxr', 1, 1, 0), ('mxr', 1, 1, 3), ('fin', 0, 0, 4, 0, 128), ('mxr', 1, 3, 2), ('mxr', 1, 0, 1), ('mxr', 1, 2, 0), ('mxr', 1, 3, 1), ('mxr', 1, 3, 0), ('mxr', 1, 2, 2), ('fin', 1, 0, 2, 0, 128), ('mxr', 1, 2, 3), ('mxr', 1, 2, 1), ('lm', 1, 3, 4, 0, 128, 'v'), ('lm', 1, 2, 3, 0, 128, 'v'), ('fin', 1, 3, 4, 0, 128), ('fin', 1, 2, 3, 0, 128)]
        pool = [('lm', 0, 0, 4, 0, 128, 'g'), ('lm', 1, 0, 2, 0, 128, 'g')]
        sp = [('st', 0, 0, 4), ('st', 1, 0, 2), ('st', 1, 2, 4)]

        fns = dict(wp=wp, wsp=wsp, tr=tr, xc=xc, xq=xq, mx1=mx1, relu=relu, hi=hi, hq=hq, si=si, sq=sq, ui=ui, uq=uq, mxu=mxu, ucp=ucp, utr=utr, mx2=mx2, mxr=mxr, lm=lm, fin=fin, st=st, bperm=bperm, btr=btr, bcopy=bcopy, ltr=ltr, lcopy=lcopy, dm=dm)

        def strip(n):
            return n[:-1] if n[0] in ("xc", "si", "ui", "lm", "hi", "bcopy") else n

        tr_ring, acc_ring = [], []
        for n in pe:
            if n[0] == "tr":
                tr_ring.append((n, [("xc",) + n[1:]]))
            elif n[0] == "btr":
                tr_ring.append((n, [("bcopy",)]))
            elif n[0] == "ltr":
                tr_ring.append((n, [("lcopy",)]))
            elif n[0] == "dm":
                tr_ring.append((n, []))
            elif n[0] == "utr":
                tr_ring.append((n, [m for m in dve if m[:2] == ("fin", n[1])]))
            elif n[0] == "mx1" and n[4] == 0:
                acc_ring.append((n, [("relu",) + n[1:4]]))
            elif n[0] == "mx2":
                acc_ring.append((n, [("mxr",) + n[1:]]))
            elif n[0] == "mxu":
                acc_ring.append((n, [("ucp",) + n[1:]]))
        ring_need = {}
        for ring, bufs in ((tr_ring, TRB), (acc_ring, ACB)):
            for i in range(bufs, len(ring)):
                ring_need[ring[i][0]] = ring[i - bufs][1]

        raw_order = []
        for n in act:
            if n[0] == "relu" and n[1:3] not in raw_order:
                raw_order.append(n[1:3])
        in_order = [n[1:] for n in dve if n[0] == "hq"]

        def needs(n):
            k = n[0]
            r = list(ring_need.get(n, []))
            if k == "xc":
                r += [("tr",) + n[1:4]]
            elif k == "xq":
                r += [("xc", n[1], g, rp) for g in range(n[2], n[2] + n[3]) for rp in range(2)]
            elif k == "mx1":
                r += [m for m in dve if m[0] == "xq" and m[1] == n[1] and m[2] <= n[4] < m[2] + m[3]] + [("wp", n[2]), ("wsp",)]
            elif k == "relu":
                r += [("mx1", n[1], n[2], n[3], 3), ("bcopy",)] + [("hi",) + m for m in raw_order[: max(0, raw_order.index(n[1:3]) - 1)]]
            elif k == "hi":
                r += [("relu", n[1], n[2], t) for t in range(T)] + [("hq",) + m for m in in_order[: max(0, in_order.index(n[1:3]) - 1)]] + [("hi",) + m for m in in_order[: in_order.index(n[1:3])]]
            elif k == "hq":
                r += [("hi", n[1], n[2])]
            elif k == "sq":
                r += [m[:-1] for m in act + dve + pool if m[0] == "si" and m[1] == n[1] and m[2] == n[2] // 2]
            elif k == "uq":
                r += [("ui",)]
            elif k == "mxu":
                r += [("hq", n[1], 0), ("hq", n[1], 1), ("uq",)]
            elif k == "ucp":
                r += [("mxu", n[1])]
            elif k == "utr":
                r += [("ucp", n[1])]
            elif k == "mx2":
                r += [("hq", n[1], 0), ("hq", n[1], 1), ] + [m for m in dve if m[0] == "sq" and m[2] <= n[3] < m[2] + m[3]]
            elif k == "mxr":
                r += [("mx2",) + n[1:]]
            elif k == "lm":
                r += [("mxr", n[1], a, q) for a in range(n[2], n[3]) for q in range(n[4] // 32, n[5] // 32)] + [("lcopy",)]
            elif k == "fin":
                lms = [m[:-1] for m in dve + pool if m[0] == "lm" and m[1] == n[1] and m[2] < n[3] and m[3] > n[2] and m[4] < n[5] and m[5] > n[4]]
                assert lms
                r += lms + [("utr", n[1])]
            elif k == "st":
                r += [m for m in dve if m[0] == "fin" and m[1] == n[1] and m[2] < n[3] and m[3] > n[2]]
            elif k == "bcopy":
                r += [("btr",)]
            elif k == "btr":
                r += [("bperm",)]
            elif k == "lcopy":
                r += [("ltr",)]
            return r

        done = set()
        order = [list(pe), list(act), list(dve), list(pool), list(sp)]
        while any(order):
            moved = False
            for q in order:
                while q and all(n in done for n in needs(q[0])):
                    name = q.pop(0)
                    fns[name[0]](*name[1:])
                    done.add(strip(name))
                    moved = True
            assert moved, [q[0] for q in order if q]
